import numpy as np
import ml_dtypes


def mxq(x, axis, fmt="e4m3"):
    dtype, down = {"e4m3": (ml_dtypes.float8_e4m3fn, 7), "e5m2": (ml_dtypes.float8_e5m2, 14)}[fmt]
    v = np.moveaxis(np.asarray(x, np.float32).astype(ml_dtypes.bfloat16).astype(np.float64), axis, -1)
    blocks = v.reshape(v.shape[:-1] + (-1, 32))
    amax = np.abs(blocks).max(-1, keepdims=True)
    byte = np.maximum(np.where(amax > 0, np.frexp(amax)[1] - 1 + 127, 0) - down, 1)
    scale = np.exp2(byte - 127.0)
    codes = (blocks / scale).astype(np.float32).astype(dtype).astype(np.float64)
    return np.moveaxis((codes * scale).reshape(v.shape), -1, axis)


WIDE = False


def mx_kscale(k):
    if not WIDE:
        return np.ones(k)
    levels = np.array([10, -10, 5, -5, 0])
    if k % 512:
        return np.exp2(np.random.permutation(np.resize(levels, k // 32))).repeat(32)
    a = np.empty((k // 512, 16))
    for p in range(k // 512):
        a[p, :8] = np.random.permutation(np.resize(levels, 8))
        for g in range(8):
            far = levels[np.abs(levels - a[p, g]) >= 10]
            a[p, g + 8] = far[np.random.randint(len(far))]
    return np.exp2(a.ravel()).repeat(32)


def f64(x):
    return np.asarray(x).astype(np.float64)


def striped(idx):
    return np.tile(idx.reshape(-1, 16).T, (8, 1)).astype(np.uint16)


def unstriped(offs):
    return offs[:16].T.reshape(-1).astype(np.int64)


E2M1 = np.array([0.0, 0.5, 1.0, 1.5, 2.0, 3.0, 4.0, 6.0, -0.0, -0.5, -1.0, -1.5, -2.0, -3.0, -4.0, -6.0])


def pack_weight(w, fmt):
    k, n = w.shape
    w = f64(np.asarray(w, np.float32).astype(ml_dtypes.bfloat16)).reshape(k // 32, 32, n)
    amax = np.abs(w).max(1)
    if fmt == "e4m3":
        byte = np.frexp(amax)[1] - 1 + 127 - 7
    else:
        mant, ex = np.frexp(amax / 6.0)
        byte = np.where(mant > 0.5, ex, ex - 1) + 127
    byte = np.clip(np.where(amax > 0, byte, 1), 1, 254)
    scaled = (w * np.exp2(127.0 - byte)[:, None, :]).reshape(k, n).astype(np.float32)
    by_word = np.ascontiguousarray(scaled.reshape(k // 512, 128, 4, n).transpose(0, 1, 3, 2))
    if fmt == "e4m3":
        words = by_word.astype(ml_dtypes.float8_e4m3fn).view(np.uint8)
    else:
        c = by_word.astype(ml_dtypes.float4_e2m1fn).view(np.uint8) & 0xF
        words = (c[..., 0::2] | (c[..., 1::2] << 4)).reshape(k // 512, 128, 2 * n)
    return np.ascontiguousarray(words), np.ascontiguousarray(byte.astype(np.uint8).reshape(k // 512, 16, n))


def unpack_weight(words, scales, fmt):
    g, _, n = scales.shape
    words = np.ascontiguousarray(words).reshape(g, 128, n, -1)
    if fmt == "e4m3":
        vals = words.view(ml_dtypes.float8_e4m3fn).astype(np.float64)
    else:
        nib = np.empty((g, 128, n, 4), np.uint8)
        nib[..., 0::2] = words & 0xF
        nib[..., 1::2] = words >> 4
        vals = E2M1[nib]
    vals = vals * np.repeat(np.exp2(scales.astype(np.float64) - 127.0), 8, axis=1)[..., None]
    return vals.transpose(0, 1, 3, 2).reshape(g * 512, n)


def gelu(v):
    return 0.5 * v * (1.0 + np.tanh(np.sqrt(2.0 / np.pi) * (v + 0.044715 * v**3)))


K, T, S, T2, H, N = 1024, 2048, 512, 1024, 1024, 512


def setup_inputs():
    n = np.random.standard_normal
    s = mx_kscale(K)[:, None]
    u = mx_kscale(H)[:, None]
    tab_words, tab_scales = pack_weight(n((K, T)) * s, "e4m3")
    tab2_words, tab2_scales = pack_weight(n((K, T)) * s, "e4m3")
    w3_words, w3_scales = pack_weight(0.9 * n((K, H)) / np.sqrt(K) / s * u.T, "e4m3")
    w4_words, w4_scales = pack_weight(n((H, N)) / np.sqrt(H) / u, "e2m1")
    return {
        "tab_words": tab_words, "tab_scales": tab_scales,
        "tab2_words": tab2_words, "tab2_scales": tab2_scales,
        "offs": striped(np.random.permutation(T)[:S]),
        "offs2": striped(np.random.permutation(T)[:S]),
        "offs3": striped(np.random.permutation(T2)[:S]),
        "offs4": striped(np.random.permutation(T2)[:S]),
        "w1": (1.2 * n((K, H)) / np.sqrt(K) / s).astype(np.float32),
        "w2": (0.55 * n((K, H)) / np.sqrt(K) / s).astype(np.float32),
        "gain": (2.0 * np.exp(0.2 * n(H)) * u[:, 0]).astype(np.float32),
        "w3_words": w3_words, "w3_scales": w3_scales,
        "wg1": np.exp(0.3 * n((128, S))).astype(np.float32),
        "wg2": np.exp(0.3 * n((128, S))).astype(np.float32),
        "lib": (0.7 * n((H, T2)) * u).astype(np.float32),
        "w4_words": w4_words, "w4_scales": w4_scales,
    }


def reference(tab_words, tab_scales, tab2_words, tab2_scales, offs, offs2, offs3, offs4,
              w1, w2, gain, w3_words, w3_scales, wg1, wg2, lib, w4_words, w4_scales):
    v = unpack_weight(tab_words, tab_scales, "e4m3")[:, unstriped(offs)]
    v2 = unpack_weight(tab2_words, tab2_scales, "e4m3")[:, unstriped(offs2)]
    d = mxq(f64(w1), 0, "e4m3").T @ v
    b = mxq(f64(w2), 0, "e4m3").T @ v
    h1 = (np.tanh(d) + np.sin(b)) * f64(gain)[:, None]
    h2 = np.abs(unpack_weight(w3_words, w3_scales, "e4m3").T @ v2)
    pa = np.zeros((H, T2))
    pa[:, unstriped(offs3)] = np.tile(f64(wg1), (H // 128, 1)) * h1
    pb = np.zeros((H, T2))
    pb[:, unstriped(offs4)] = np.tile(f64(wg2), (H // 128, 1)) * h2
    z = np.minimum(pa, f64(lib)) + np.maximum(pb, f64(lib))
    return unpack_weight(w4_words, w4_scales, "e2m1").T @ mxq(z, 0, "e4m3")

@@ -1,0 +1,382 @@
+import math
+from contextlib import ExitStack
+
+import concourse.mybir as mybir
+from concourse.masks import make_identity
+
+K, T, S, T2, H, N = 1024, 2048, 512, 1024, 1024, 512
+FLOPS = 2 * (3 * K * H * S + H * N * T2)
+
+F32 = mybir.dt.float32
+BF16 = mybir.dt.bfloat16
+I32 = mybir.dt.int32
+U32 = mybir.dt.uint32
+U16 = mybir.dt.uint16
+U8 = mybir.dt.uint8
+FP8X4 = mybir.dt.float8_e4m3fn_x4
+FP4X4 = mybir.dt.float4_e2m1fn_x4
+ALU = mybir.AluOpType
+ACT = mybir.ActivationFunctionType
+
+P = 128
+PASSES = 2
+SLICES = H // P
+HALF = 512
+CHUNK = 256
+CHUNKS = T2 // CHUNK
+LAG = 2
+ROUNDER = 1.5 * 2.0**23
+TWO_PI = 2.0 * math.pi
+
+
+def tile_list_mineral_outcrop_score_kernel(
+    tc, tab_words, tab_scales, tab2_words, tab2_scales, offs, offs2, offs3, offs4,
+    w1, w2, gain, w3_words, w3_scales, wg1, wg2, lib, w4_words, w4_scales, out,
+):
+    nc = tc.nc
+    with ExitStack() as ctx:
+        lists = ctx.enter_context(tc.tile_pool(name="lists", bufs=1))
+        keep = ctx.enter_context(tc.tile_pool(name="keep", bufs=1))
+        ring = ctx.enter_context(tc.tile_pool(name="ring", bufs=1))
+        psum = ctx.enter_context(tc.psum_pool(name="psum", bufs=1))
+
+        def load_list(source, name):
+            tile = lists.tile([P, S // 16], U16, name=name)
+            nc.sync.dma_start(tile[:], source)
+            return tile
+
+        def bank(tag, shape):
+            return psum.tile(shape, F32, name=tag, tag=tag)
+
+        def load_plane(queue, plane, scales):
+            for q in range(4):
+                queue.dma_start(
+                    plane[32 * q : 32 * q + 4 * PASSES, :].bitcast(I32),
+                    scales[:, 4 * q : 4 * q + 4, :].bitcast(I32),
+                )
+
+        def load_words(tile, words, a):
+            nc.sync.dma_start(tile[:].bitcast(I32), words[a].rearrange("p t i -> p (t i)").bitcast(I32))
+
+        tab2_plane = keep.tile([P, T], U8, align_bytes=64)
+        w3_plane = keep.tile([P, H], U8, align_bytes=64)
+        tab_plane = keep.tile([P, T], U8, align_bytes=64)
+        w4_plane = keep.tile([P, PASSES, N], U8, align_bytes=64)
+        pb = [keep.tile([P, T2], F32, name="pb%d" % s) for s in range(SLICES)]
+        pa = [keep.tile([P, T2], F32, name="pa%d" % s) for s in range(2)]
+        nc.vector.memset(tab2_plane[:].bitcast(I32), 0)
+        nc.vector.memset(w3_plane[:].bitcast(I32), 0)
+        nc.vector.memset(tab_plane[:].bitcast(I32), 0)
+        for s in range(2):
+            nc.vector.memset(pb[s][:].bitcast(I32), 0)
+
+        def table_tile(a):
+            return ring.tile([P, T], U32, name="table", tag="table%d" % a, align_bytes=64)
+
+        def raw_tile(shape, dtype):
+            return ring.tile(shape, dtype, name="raw", tag="raw", bufs=4, align_bytes=64)
+
+        w3_c, w3_s = {}, {}
+
+        def load_w3(g):
+            raw = ring.tile([P, PASSES, HALF], I32, name="w3_raw", tag="grouped%d" % g, align_bytes=64)
+            words = w3_words.rearrange("a p c i -> p a (c i)")[:, :, 4 * HALF * g : 4 * HALF * (g + 1)]
+            nc.sync.dma_start(raw[:], words.bitcast(I32))
+            return raw
+
+        def deal_w3(g, raw):
+            w3_c[g] = keep.tile([P, PASSES, HALF], I32, name="w3_c%d" % g, align_bytes=64)
+            w3_s[g] = keep.tile([P, HALF], U8, name="w3_s%d" % g, align_bytes=64)
+            nc.vector.tensor_copy(
+                w3_c[g][:].rearrange("p a (t c i) -> p a c t i", t=4, i=4),
+                raw[:].rearrange("p a (c i t) -> p a c t i", t=4, i=4),
+            )
+            nc.vector.tensor_copy(
+                w3_s[g][:].rearrange("p (t q) -> p t q", t=4),
+                w3_plane[:, HALF * g : HALF * (g + 1)].rearrange("p (q t) -> p t q", t=4),
+            )
+
+        def load_wg(tile, wg, t0, t1):
+            rows = wg.rearrange("(q t) j -> q (t j)", t=4)[:, t0 * S : t1 * S]
+            nc.sync.dma_start(
+                tile[:, t0:t1, :].rearrange("p t j -> p (t j)"),
+                rows.unsqueeze(0).broadcast_to([4, 32, (t1 - t0) * S]),
+            )
+
+        tab2_w = [table_tile(a) for a in range(PASSES)]
+        load_words(tab2_w[0], tab2_words, 0)
+        idx2 = load_list(offs2, "idx2")
+        load_plane(nc.sync, tab2_plane, tab2_scales)
+        w3_raw = load_w3(0)
+        load_words(tab2_w[1], tab2_words, 1)
+        load_plane(nc.sync, w3_plane, w3_scales)
+        idx4 = load_list(offs4, "idx4")
+        wg2_sb = keep.tile([P, 4, S], F32)
+        load_wg(wg2_sb, wg2, 0, 1)
+        w3_raw1 = load_w3(1)
+        load_wg(wg2_sb, wg2, 1, 4)
+        for s in range(2, SLICES):
+            nc.gpsimd.memset(pb[s][:].bitcast(I32), 0)
+        ident = keep.tile([P, P], F32)
+        make_identity(nc, ident[:])
+        gain_sb = keep.tile([P, 2, 4], F32)
+        nc.gpsimd.dma_start(gain_sb[:], gain.rearrange("(g q t) -> q g t", g=2, t=4))
+        for page in pa:
+            nc.gpsimd.memset(page[:].bitcast(I32), 0)
+        nc.gpsimd.memset(w4_plane[:].bitcast(I32), 0)
+        deal_w3(0, w3_raw)
+
+        def gather(words, plane, idx, name):
+            codes = [keep.tile([P, S], U32, name="%s_c%d" % (name, a), align_bytes=64) for a in range(PASSES)]
+            scales = keep.tile([P, S], U8, name=name + "_s", align_bytes=64)
+            nc.vector.tensor_copy(codes[0][:], words[0][:].indirect(idx[:]))
+            nc.vector.tensor_copy(scales[:], plane[:].indirect(idx[:]))
+            nc.vector.tensor_copy(codes[1][:], words[1][:].indirect(idx[:]))
+            return codes, scales
+
+        v2_c, v2_s = gather(tab2_w, tab2_plane, idx2, "v2")
+        deal_w3(1, w3_raw1)
+
+        def thermal(s):
+            h, c0 = divmod(s * P, HALF)
+            acc = bank("bd"[s % 2] + "0" if s < 4 else "h0", [P, S])
+            for a in range(PASSES):
+                nc.tensor.matmul_mx(
+                    out=acc[:],
+                    lhsT=w3_c[h][:, a, c0 : c0 + P].bitcast(FP8X4),
+                    lhsT_scale=w3_s[h][4 * a :, c0 : c0 + P],
+                    rhs=v2_c[a][:].bitcast(FP8X4),
+                    rhs_scale=v2_s[4 * a :, :],
+                    start=(a == 0),
+                    stop=(a == PASSES - 1),
+                )
+            if s == 4:
+                h2 = ring.tile([P, S], F32, name="feat", tag="grouped2", align_bytes=64)
+            else:
+                h2 = ring.tile([P, S], F32, name="feat", tag="feat", bufs=6)
+            nc.scalar.activation(h2[:], acc[:], ACT.Abs)
+            nc.vector.tensor_tensor(pb[s][:].indirect(idx4[:]), h2[:], wg2_sb[:, s % 4, :], ALU.mult)
+
+        for s in range(SLICES // 2):
+            thermal(s)
+
+        w_c, w_s = {}, {}
+        order = [(1, 0), (0, 0), (1, 1), (0, 1)]
+
+        def load_weight(k, h):
+            m, a = order[k]
+            w = (w1, w2)[m]
+            raw = raw_tile([P, 4, HALF], F32)
+            rows = w[512 * a : 512 * (a + 1), HALF * h : HALF * (h + 1)]
+            nc.sync.dma_start(raw[:], rows.rearrange("(p j) c -> p j c", j=4))
+            return raw
+
+        def quantise_weight(k, h, raw):
+            m, a = order[k]
+            grouped = ring.tile([P, 4, P, 4], BF16, name="grouped", tag="grouped%d" % k, align_bytes=64)
+            for q0 in range(0, P, P // 2):
+                nc.scalar.copy(
+                    grouped[:, :, q0 : q0 + P // 2, :].rearrange("p t q j -> p q j t"),
+                    raw[:, :, 4 * q0 : 4 * q0 + 2 * P].rearrange("p j (q t) -> p q j t", t=4),
+                )
+            w_c[m, h, a] = keep.tile([P, HALF], U32, name="w_c%d%d%d" % (m, h, a), align_bytes=64)
+            w_s[m, h, a] = keep.tile([P, HALF], U8, name="w_s%d%d%d" % (m, h, a), align_bytes=64)
+            nc.vector.quantize_mx(
+                out=w_c[m, h, a][:].bitcast(FP8X4),
+                scales=w_s[m, h, a][:],
+                in_=grouped[:].rearrange("p t q j -> p (t q j)"),
+            )
+
+        raws = [load_weight(0, 0)]
+        idx1 = load_list(offs, "idx1")
+        tab_w = [table_tile(a) for a in range(PASSES)]
+        load_words(tab_w[0], tab_words, 0)
+        load_plane(nc.sync, tab_plane, tab_scales)
+        raws.append(load_weight(1, 0))
+        load_words(tab_w[1], tab_words, 1)
+        raws.append(load_weight(2, 0))
+        raws.append(load_weight(3, 0))
+        v_c, v_s = gather(tab_w, tab_plane, idx1, "v")
+        for k in range(4):
+            quantise_weight(k, 0, raws[k])
+        for s in range(SLICES // 2, SLICES):
+            thermal(s)
+        wg1_sb = keep.tile([P, 4, S], F32)
+        load_wg(wg1_sb, wg1, 0, 4)
+        idx3 = load_list(offs3, "idx3")
+
+        lib_sb = {}
+
+        def load_lib(s):
+            lib_sb[s] = ring.tile([P, T2], F32, name="lib_sb", tag="lib_sb", bufs=4)
+            nc.sync.dma_start(lib_sb[s][:], lib.rearrange("(g q t) m -> g t q m", g=2, t=4)[s // 4, s % 4])
+
+        def add_transposed(dst, first, second):
+            nc.tensor.matmul(dst, lhsT=first, rhs=ident[:], start=True, stop=False, is_transpose=True)
+            nc.tensor.matmul(dst, lhsT=second, rhs=ident[:], start=False, stop=True, is_transpose=True)
+
+        h1 = {}
+
+        def shortwave(s):
+            h, c0 = divmod(s * P, HALF)
+            cols = slice(c0, c0 + P)
+            b_acc = bank("b%d" % (s % 2), [P, S])
+            for a in range(PASSES):
+                nc.tensor.matmul_mx(
+                    out=b_acc[:],
+                    lhsT=w_c[1, h, a][:, cols].bitcast(FP8X4),
+                    lhsT_scale=w_s[1, h, a][:, cols],
+                    rhs=v_c[a][:].bitcast(FP8X4),
+                    rhs_scale=v_s[4 * a :, :],
+                    start=(a == 0),
+                    stop=(a == PASSES - 1),
+                )
+            d_acc = bank("d%d" % (s % 2), [P, 4, P])
+            for j in range(4):
+                for a in range(PASSES):
+                    nc.tensor.matmul_mx(
+                        out=d_acc[:, j, :],
+                        lhsT=v_c[a][:, j * P : (j + 1) * P].bitcast(FP8X4),
+                        lhsT_scale=v_s[4 * a :, j * P : (j + 1) * P],
+                        rhs=w_c[0, h, a][:, cols].bitcast(FP8X4),
+                        rhs_scale=w_s[0, h, a][:, cols],
+                        start=(a == 0),
+                        stop=(a == PASSES - 1),
+                    )
+            shifted = ring.tile([P, S], U32, name="shifted", tag="shifted", bufs=1)
+            turns = ring.tile([P, S], F32, name="turns", tag="turns", bufs=2)
+            whole = ring.tile([P, S], F32, name="whole", tag="whole", bufs=2)
+            nc.scalar.activation(shifted[:], b_acc[:], ACT.Copy, bias=ROUNDER, scale=1.0 / TWO_PI)
+            nc.scalar.activation(turns[:], b_acc[:], ACT.Copy, scale=1.0 / TWO_PI)
+            nc.scalar.activation(whole[:], shifted[:], ACT.Copy, bias=ROUNDER, scale=-1.0)
+            both = ring.tile([P, 2, S], F32, name="both", tag="x%d" % (s % 2))
+            nc.scalar.activation(both[:, 0, :], d_acc[:].rearrange("p j r -> p (j r)"), ACT.Tanh)
+            r_acc = bank("r%d" % (s % 2), [P, 4, P])
+            for j in range(4):
+                add_transposed(r_acc[:, j, :], turns[:, j * P : (j + 1) * P], whole[:, j * P : (j + 1) * P])
+            nc.scalar.activation(both[:, 1, :], r_acc[:].rearrange("p j r -> p (j r)"), ACT.Sin, scale=TWO_PI)
+            h_acc = bank("h%d" % (s % 2), [P, S])
+            for j in range(4):
+                add_transposed(h_acc[:, j * P : (j + 1) * P], both[:, 0, j * P : (j + 1) * P], both[:, 1, j * P : (j + 1) * P])
+            h1[s] = ring.tile([P, S], F32, name="feat", tag="feat", bufs=6)
+            nc.scalar.activation(h1[s][:], h_acc[:], ACT.Copy, scale=gain_sb[:, s // 4, s % 4 : s % 4 + 1])
+
+        w4_w = keep.tile([P, PASSES, 2 * N], U8, align_bytes=64)
+        z_t, z_c, z_s = {}, {}, {}
+
+        def quantise_z(g, c, z_in):
+            z_c[g, c] = keep.tile([P, CHUNK], U32, name="z_c%d%d" % (g, c), align_bytes=64)
+            z_s[g, c] = keep.tile([P, CHUNK], U8, name="z_s%d%d" % (g, c), align_bytes=64)
+            nc.vector.quantize_mx(out=z_c[g, c][:].bitcast(FP8X4), scales=z_s[g, c][:], in_=z_in[:])
+
+        def z_tile():
+            return ring.tile([P, 4 * CHUNK], BF16, name="z_in", tag="z_in", bufs=2, align_bytes=64)
+
+        def sum_pair(u):
+            for c in range(CHUNKS):
+                if u == 0:
+                    z_t[c] = ring.tile([P, 2, 2, P, 2], BF16, name="z_t", tag="z_t%d" % c, align_bytes=64)
+                z_acc = bank("z%d" % (c % 2), [P, 2, 2, P])
+                for a in range(2):
+                    cols = slice(c * CHUNK + a * P, c * CHUNK + (a + 1) * P)
+                    for e in range(2):
+                        add_transposed(z_acc[:, a, e, :], lower[2 * u + e][:, cols], upper[2 * u + e][:, cols])
+                nc.scalar.copy(z_t[c][:, :, u, :, :], z_acc[:].rearrange("m a e p -> m a p e"))
+                if u == 1:
+                    words = z_t[c][:].rearrange("m a u p e -> m (a u p e)").bitcast(F32)
+                    w_acc = bank("w%d" % (c % 2), [P, 2, 2, P])
+                    for a in range(2):
+                        for v in range(2):
+                            nc.tensor.transpose(w_acc[:, a, v, :], words[:, (2 * a + v) * P : (2 * a + v + 1) * P], ident[:])
+                    z_in = z_tile()
+                    nc.scalar.copy(
+                        z_in[:].bitcast(F32).rearrange("p (a m u) -> p a m u", a=2, u=2),
+                        w_acc[:].rearrange("p a u m -> p a m u"),
+                    )
+                    quantise_z(0, c, z_in)
+
+        def scores(c):
+            for half in range(2):
+                acc = bank("brdh"[c] + "%d" % half, [P, 2, CHUNK])
+                for i in range(2):
+                    n0 = (2 * half + i) * P
+                    for g in range(PASSES):
+                        nc.tensor.matmul_mx(
+                            out=acc[:, i, :],
+                            lhsT=w4_w[:, g, 2 * n0 : 2 * (n0 + P)].bitcast(FP4X4),
+                            lhsT_scale=w4_plane[:, g, n0 : n0 + P],
+                            rhs=z_c[g, c][:].bitcast(FP8X4),
+                            rhs_scale=z_s[g, c][:],
+                            start=(g == 0),
+                            stop=(g == PASSES - 1),
+                        )
+                staged = ring.tile([P, 2, CHUNK], F32, name="staged", tag=("turns", "whole")[half], bufs=2)
+                if half == 0 and c == CHUNKS - 1:
+                    nc.vector.tensor_copy(staged[:], acc[:])
+                else:
+                    nc.scalar.copy(staged[:], acc[:])
+                rows = out[2 * half * P : 2 * (half + 1) * P, c * CHUNK : (c + 1) * CHUNK]
+                nc.sync.dma_start(rows.rearrange("(i p) m -> p i m", p=P), staged[:])
+
+        lower, upper, lower4, upper4 = {}, {}, {}, {}
+
+        def wide_tile(on_table, k):
+            if on_table:
+                return ring.tile([P, 4, HALF], F32, name="wide", tag="table%d" % k, align_bytes=64)
+            return raw_tile([P, 4, HALF], F32)
+
+        def place(s):
+            g, t = divmod(s, 4)
+            page = pa[s % 2]
+            nc.vector.tensor_tensor(page[:].indirect(idx3[:]), h1[s][:], wg1_sb[:, t, :], ALU.mult)
+            if g < 0:
+                upper[s] = ring.tile([P, T2], F32, name="upper", tag="upper", bufs=3)
+                nc.vector.tensor_tensor(upper[s][:], pb[s][:], lib_sb[s][:], ALU.max)
+                lower[s] = ring.tile([P, T2], F32, name="lower", tag="x%d" % ((s + LAG) % 2))
+                nc.vector.tensor_tensor(lower[s][:], page[:], lib_sb[s][:], ALU.min)
+                if t % 2 == 1:
+                    sum_pair(t // 2)
+                return
+            for k in range(2):
+                cols = slice(k * HALF, (k + 1) * HALF)
+                if t == 0:
+                    upper4[k] = wide_tile(True, k)
+                nc.vector.tensor_tensor(upper4[k][:, t, :], pb[s][:, cols], lib_sb[s][:, cols], ALU.max)
+            for k in range(2):
+                cols = slice(k * HALF, (k + 1) * HALF)
+                if t == 0:
+                    lower4[k] = wide_tile(False, k)
+                nc.vector.tensor_tensor(lower4[k][:, t, :], page[:, cols], lib_sb[s][:, cols], ALU.min)
+            if t == 3:
+                for c in range(CHUNKS):
+                    k, m0 = divmod(c * CHUNK, HALF)
+                    z_in = z_tile()
+                    nc.vector.tensor_tensor(
+                        z_in[:].rearrange("p (c i t) -> p c t i", t=4, i=4),
+                        lower4[k][:, :, m0 : m0 + CHUNK].rearrange("p t (c i) -> p c t i", i=4),
+                        upper4[k][:, :, m0 : m0 + CHUNK].rearrange("p t (c i) -> p c t i", i=4),
+                        ALU.add,
+                    )
+                    quantise_z(g, c, z_in)
+                    if g == PASSES - 1:
+                        scores(c)
+
+        for s in range(SLICES + LAG):
+            if s < 4:
+                load_lib(s)
+            if s < SLICES:
+                shortwave(s)
+            if s < 2:
+                for k in (2 * s, 2 * s + 1):
+                    quantise_weight(k, 1, load_weight(k, 1))
+            if s == 3:
+                nc.sync.dma_start(w4_w[:].bitcast(I32), w4_words.rearrange("a p c -> p a c").bitcast(I32))
+                for q in range(4):
+                    nc.sync.dma_start(
+                        w4_plane[32 * q : 32 * q + 4, :, :].bitcast(I32),
+                        w4_scales[:, 4 * q : 4 * q + 4, :].rearrange("a r n -> r a n").bitcast(I32),
+                    )
+            if s >= LAG:
+                place(s - LAG)
+                if s - LAG + 4 < SLICES:
+                    load_lib(s - LAG + 4)

@@ -67,8 +67,11 @@ def tile_list_mineral_outcrop_score_kernel(
         nc.vector.memset(tab2_plane[:].bitcast(I32), 0)
         nc.vector.memset(w3_plane[:].bitcast(I32), 0)
         nc.vector.memset(tab_plane[:].bitcast(I32), 0)
-        for s in range(2):
+        for s in range(6):
             nc.vector.memset(pb[s][:].bitcast(I32), 0)
+        warm = keep.tile([P, 16], F32)
+        nc.gpsimd.memset(warm[:, 0:1], 0.0)
+        nc.scalar.activation(warm[:, 8:9], warm[:, 0:1], ACT.Silu)
 
         def table_tile(a):
             return ring.tile([P, T], U32, name="table", tag="table%d" % a, align_bytes=64)
@@ -96,13 +99,13 @@ def tile_list_mineral_outcrop_score_kernel(
                 w3_plane[:, HALF * g : HALF * (g + 1)].rearrange("p (q t) -> p t q", t=4),
             )
 
-        def load_wg(tile, wg, t0, t1):
+        def load_wg(queue, tile, wg, t0, t1):
             rows = wg.rearrange("(q t) j -> q (t j)", t=4)[:, t0 * S : t1 * S]
-            nc.sync.dma_start(
-                tile[:, t0:t1, :].rearrange("p t j -> p (t j)"),
-                rows.unsqueeze(0).broadcast_to([4, 32, (t1 - t0) * S]),
-            )
+            for q in range(4):
+                queue.dma_start(tile[32 * q : 32 * (q + 1), t0:t1, :].rearrange("p t j -> p (t j)"), rows)
 
+        wg2_sb = keep.tile([P, 4, S], F32)
+        load_wg(nc.gpsimd, wg2_sb, wg2, 0, 1)
         tab2_w = [table_tile(a) for a in range(PASSES)]
         load_words(tab2_w[0], tab2_words, 0)
         idx2 = load_list(offs2, "idx2")
@@ -111,11 +114,9 @@ def tile_list_mineral_outcrop_score_kernel(
         load_words(tab2_w[1], tab2_words, 1)
         load_plane(nc.sync, w3_plane, w3_scales)
         idx4 = load_list(offs4, "idx4")
-        wg2_sb = keep.tile([P, 4, S], F32)
-        load_wg(wg2_sb, wg2, 0, 1)
         w3_raw1 = load_w3(1)
-        load_wg(wg2_sb, wg2, 1, 4)
-        for s in range(2, SLICES):
+        load_wg(nc.sync, wg2_sb, wg2, 1, 4)
+        for s in range(6, SLICES):
             nc.gpsimd.memset(pb[s][:].bitcast(I32), 0)
         ident = keep.tile([P, P], F32)
         make_identity(nc, ident[:])
@@ -202,7 +203,6 @@ def tile_list_mineral_outcrop_score_kernel(
         for s in range(SLICES // 2, SLICES):
             thermal(s)
         wg1_sb = keep.tile([P, 4, S], F32)
-        load_wg(wg1_sb, wg1, 0, 4)
         idx3 = load_list(offs3, "idx3")
 
         lib_sb = {}
@@ -295,21 +295,27 @@ def tile_list_mineral_outcrop_score_kernel(
                     )
                     quantise_z(0, c, z_in)
 
+        score_acc = {}
+
+        def scores_pass(g, c, half):
+            if g == 0:
+                score_acc[c, half] = bank("brdh"[c] + "%d" % half, [P, 2, CHUNK])
+            for i in range(2):
+                n0 = (2 * half + i) * P
+                nc.tensor.matmul_mx(
+                    out=score_acc[c, half][:, i, :],
+                    lhsT=w4_w[:, g, 2 * n0 : 2 * (n0 + P)].bitcast(FP4X4),
+                    lhsT_scale=w4_plane[:, g, n0 : n0 + P],
+                    rhs=z_c[g, c][:].bitcast(FP8X4),
+                    rhs_scale=z_s[g, c][:],
+                    start=(g == 0 and i == 0),
+                    stop=(g == PASSES - 1 and i == 1),
+                )
+
         def scores(c):
             for half in range(2):
-                acc = bank("brdh"[c] + "%d" % half, [P, 2, CHUNK])
-                for i in range(2):
-                    n0 = (2 * half + i) * P
-                    for g in range(PASSES):
-                        nc.tensor.matmul_mx(
-                            out=acc[:, i, :],
-                            lhsT=w4_w[:, g, 2 * n0 : 2 * (n0 + P)].bitcast(FP4X4),
-                            lhsT_scale=w4_plane[:, g, n0 : n0 + P],
-                            rhs=z_c[g, c][:].bitcast(FP8X4),
-                            rhs_scale=z_s[g, c][:],
-                            start=(g == 0),
-                            stop=(g == PASSES - 1),
-                        )
+                scores_pass(1, c, half)
+                acc = score_acc[c, half]
                 staged = ring.tile([P, 2, CHUNK], F32, name="staged", tag=("turns", "whole")[half], bufs=2)
                 if half == 0 and c == CHUNKS - 1:
                     nc.vector.tensor_copy(staged[:], acc[:])
@@ -364,6 +370,8 @@ def tile_list_mineral_outcrop_score_kernel(
         for s in range(SLICES + LAG):
             if s < 4:
                 load_lib(s)
+            if s == 2:
+                load_wg(nc.sync, wg1_sb, wg1, 0, 4)
             if s < SLICES:
                 shortwave(s)
             if s < 2:
@@ -376,6 +384,10 @@ def tile_list_mineral_outcrop_score_kernel(
                         w4_plane[32 * q : 32 * q + 4, :, :].bitcast(I32),
                         w4_scales[:, 4 * q : 4 * q + 4, :].rearrange("a r n -> r a n").bitcast(I32),
                     )
+            if s == SLICES - 1:
+                for c in range(CHUNKS):
+                    for half in range(2):
+                        scores_pass(0, c, half)
             if s >= LAG:
                 place(s - LAG)
                 if s - LAG + 4 < SLICES:

@@ -22,9 +22,9 @@ P = 128
 PASSES = 2
 SLICES = H // P
 HALF = 512
-CHUNK = 256
-CHUNKS = T2 // CHUNK
+PIECES = [(0, 256), (256, 256), (512, 256), (768, 128), (896, 128)]
 LAG = 2
+EARLY = 3
 ROUNDER = 1.5 * 2.0**23
 TWO_PI = 2.0 * math.pi
 
@@ -56,7 +56,12 @@ def tile_list_mineral_outcrop_score_kernel(
                 )
 
         def load_words(tile, words, a):
-            nc.sync.dma_start(tile[:].bitcast(I32), words[a].rearrange("p t i -> p (t i)").bitcast(I32))
+            nc.sync.dma_start(tile[:, a, :].bitcast(I32), words[a].rearrange("p t i -> p (t i)").bitcast(I32))
+
+        def load_dealt(tile, wg, t0, t1):
+            rows = wg.rearrange("(q t) j -> q (t j)", t=4)[:, t0 * S : t1 * S]
+            for q in range(4):
+                nc.sync.dma_start(tile[32 * q : 32 * (q + 1), t0:t1, :].rearrange("p t j -> p (t j)"), rows)
 
         tab2_plane = keep.tile([P, T], U8, align_bytes=64)
         w3_plane = keep.tile([P, H], U8, align_bytes=64)
@@ -64,25 +69,28 @@ def tile_list_mineral_outcrop_score_kernel(
         w4_plane = keep.tile([P, PASSES, N], U8, align_bytes=64)
         pb = [keep.tile([P, T2], F32, name="pb%d" % s) for s in range(SLICES)]
         pa = [keep.tile([P, T2], F32, name="pa%d" % s) for s in range(2)]
-        nc.vector.memset(tab2_plane[:].bitcast(I32), 0)
         nc.vector.memset(w3_plane[:].bitcast(I32), 0)
+        nc.vector.memset(tab2_plane[:].bitcast(I32), 0)
+        ident = keep.tile([P, P], F32)
+        make_identity(nc, ident[:])
+        nc.gpsimd.memset(w4_plane[:].bitcast(I32), 0)
         nc.vector.memset(tab_plane[:].bitcast(I32), 0)
-        for s in range(6):
+        for s in range(3):
             nc.vector.memset(pb[s][:].bitcast(I32), 0)
         warm = keep.tile([P, 16], F32)
-        nc.gpsimd.memset(warm[:, 0:1], 0.0)
+        nc.vector.memset(warm[:, 0:1], 0.0)
         nc.scalar.activation(warm[:, 8:9], warm[:, 0:1], ACT.Silu)
 
-        def table_tile(a):
-            return ring.tile([P, T], U32, name="table", tag="table%d" % a, align_bytes=64)
+        def table_tile():
+            return ring.tile([P, PASSES, T], U32, name="table", tag="table", align_bytes=64)
 
-        def raw_tile(shape, dtype):
-            return ring.tile(shape, dtype, name="raw", tag="raw", bufs=4, align_bytes=64)
+        def raw_tile():
+            return ring.tile([P, 2, 4, HALF], F32, name="raw", tag="raw", bufs=2, align_bytes=64)
 
         w3_c, w3_s = {}, {}
 
         def load_w3(g):
-            raw = ring.tile([P, PASSES, HALF], I32, name="w3_raw", tag="grouped%d" % g, align_bytes=64)
+            raw = ring.tile([P, PASSES, HALF], I32, name="w3_raw", tag=("grouped0", "lib_sb")[g], bufs=(1, 4)[g], align_bytes=(64, None)[g])
             words = w3_words.rearrange("a p c i -> p a (c i)")[:, :, 4 * HALF * g : 4 * HALF * (g + 1)]
             nc.sync.dma_start(raw[:], words.bitcast(I32))
             return raw
@@ -99,80 +107,77 @@ def tile_list_mineral_outcrop_score_kernel(
                 w3_plane[:, HALF * g : HALF * (g + 1)].rearrange("p (q t) -> p t q", t=4),
             )
 
-        def load_wg(queue, tile, wg, t0, t1):
-            rows = wg.rearrange("(q t) j -> q (t j)", t=4)[:, t0 * S : t1 * S]
-            for q in range(4):
-                queue.dma_start(tile[32 * q : 32 * (q + 1), t0:t1, :].rearrange("p t j -> p (t j)"), rows)
-
-        wg2_sb = keep.tile([P, 4, S], F32)
-        load_wg(nc.gpsimd, wg2_sb, wg2, 0, 1)
-        tab2_w = [table_tile(a) for a in range(PASSES)]
-        load_words(tab2_w[0], tab2_words, 0)
+        load_plane(nc.gpsimd, w3_plane, w3_scales)
+        tab2_w = table_tile()
+        load_words(tab2_w, tab2_words, 0)
         idx2 = load_list(offs2, "idx2")
         load_plane(nc.sync, tab2_plane, tab2_scales)
-        w3_raw = load_w3(0)
-        load_words(tab2_w[1], tab2_words, 1)
-        load_plane(nc.sync, w3_plane, w3_scales)
+        w3_raw = [load_w3(0)]
+        load_words(tab2_w, tab2_words, 1)
+
+        wg2_sb = keep.tile([P, 4, S], F32)
         idx4 = load_list(offs4, "idx4")
-        w3_raw1 = load_w3(1)
-        load_wg(nc.sync, wg2_sb, wg2, 1, 4)
-        for s in range(6, SLICES):
+        load_dealt(wg2_sb, wg2, 0, 1)
+        load_dealt(wg2_sb, wg2, 1, 3)
+        for s in range(3, SLICES):
             nc.gpsimd.memset(pb[s][:].bitcast(I32), 0)
-        ident = keep.tile([P, P], F32)
-        make_identity(nc, ident[:])
         gain_sb = keep.tile([P, 2, 4], F32)
         nc.gpsimd.dma_start(gain_sb[:], gain.rearrange("(g q t) -> q g t", g=2, t=4))
         for page in pa:
             nc.gpsimd.memset(page[:].bitcast(I32), 0)
-        nc.gpsimd.memset(w4_plane[:].bitcast(I32), 0)
-        deal_w3(0, w3_raw)
+        deal_w3(0, w3_raw[0])
 
-        def gather(words, plane, idx, name):
+        def gather(words, plane, idx, name, step):
             codes = [keep.tile([P, S], U32, name="%s_c%d" % (name, a), align_bytes=64) for a in range(PASSES)]
             scales = keep.tile([P, S], U8, name=name + "_s", align_bytes=64)
-            nc.vector.tensor_copy(codes[0][:], words[0][:].indirect(idx[:]))
+            nc.vector.tensor_copy(codes[0][:], words[:, 0, :].indirect(idx[:]))
             nc.vector.tensor_copy(scales[:], plane[:].indirect(idx[:]))
-            nc.vector.tensor_copy(codes[1][:], words[1][:].indirect(idx[:]))
+            for j0 in range(0, S, step):
+                nc.vector.tensor_copy(codes[1][:, j0 : j0 + step], words[:, 1, :].indirect(idx[:, j0 // 16 : (j0 + step) // 16]))
             return codes, scales
 
-        v2_c, v2_s = gather(tab2_w, tab2_plane, idx2, "v2")
-        deal_w3(1, w3_raw1)
+        v2_c, v2_s = gather(tab2_w, tab2_plane, idx2, "v2", S // 2)
 
         def thermal(s):
-            h, c0 = divmod(s * P, HALF)
-            acc = bank("bd"[s % 2] + "0" if s < 4 else "h0", [P, S])
-            for a in range(PASSES):
-                nc.tensor.matmul_mx(
-                    out=acc[:],
-                    lhsT=w3_c[h][:, a, c0 : c0 + P].bitcast(FP8X4),
-                    lhsT_scale=w3_s[h][4 * a :, c0 : c0 + P],
-                    rhs=v2_c[a][:].bitcast(FP8X4),
-                    rhs_scale=v2_s[4 * a :, :],
-                    start=(a == 0),
-                    stop=(a == PASSES - 1),
-                )
-            if s == 4:
+            g, c0 = divmod(s * P, HALF)
+            if s == EARLY:
                 h2 = ring.tile([P, S], F32, name="feat", tag="grouped2", align_bytes=64)
             else:
                 h2 = ring.tile([P, S], F32, name="feat", tag="feat", bufs=6)
-            nc.scalar.activation(h2[:], acc[:], ACT.Abs)
-            nc.vector.tensor_tensor(pb[s][:].indirect(idx4[:]), h2[:], wg2_sb[:, s % 4, :], ALU.mult)
+            step = S // 2 if s == 0 else S
+            for j0 in range(0, S, step):
+                picked = slice(j0, j0 + step)
+                acc = bank("ab"[(s + j0 // step) % 2] + "0" if s < EARLY else "b1", [P, step])
+                for a in range(PASSES):
+                    nc.tensor.matmul_mx(
+                        out=acc[:],
+                        lhsT=w3_c[g][:, a, c0 : c0 + P].bitcast(FP8X4),
+                        lhsT_scale=w3_s[g][4 * a :, c0 : c0 + P],
+                        rhs=v2_c[a][:, picked].bitcast(FP8X4),
+                        rhs_scale=v2_s[4 * a :, picked],
+                        start=(a == 0),
+                        stop=(a == PASSES - 1),
+                    )
+                nc.scalar.activation(h2[:, picked], acc[:], ACT.Abs)
+                offsets = idx4[:, j0 // 16 : (j0 + step) // 16]
+                nc.vector.tensor_tensor(pb[s][:].indirect(offsets), h2[:, picked], wg2_sb[:, s % 4, picked], ALU.mult)
 
-        for s in range(SLICES // 2):
+        for s in range(EARLY):
             thermal(s)
 
-        w_c, w_s = {}, {}
+        w_c, w_s, raw_pair = {}, {}, {}
         order = [(1, 0), (0, 0), (1, 1), (0, 1)]
 
-        def load_weight(k, h):
+        def load_weight(k, g):
             m, a = order[k]
-            w = (w1, w2)[m]
-            raw = raw_tile([P, 4, HALF], F32)
-            rows = w[512 * a : 512 * (a + 1), HALF * h : HALF * (h + 1)]
-            nc.sync.dma_start(raw[:], rows.rearrange("(p j) c -> p j c", j=4))
+            if k % 2 == 0:
+                raw_pair[g, k // 2] = raw_tile()
+            raw = raw_pair[g, k // 2][:, k % 2]
+            rows = (w1, w2)[m][512 * a : 512 * (a + 1), HALF * g : HALF * (g + 1)]
+            nc.sync.dma_start(raw, rows.rearrange("(p j) c -> p j c", j=4))
             return raw
 
-        def quantise_weight(k, h, raw):
+        def quantise_weight(k, g, raw):
             m, a = order[k]
             grouped = ring.tile([P, 4, P, 4], BF16, name="grouped", tag="grouped%d" % k, align_bytes=64)
             for q0 in range(0, P, P // 2):
@@ -180,27 +185,28 @@ def tile_list_mineral_outcrop_score_kernel(
                     grouped[:, :, q0 : q0 + P // 2, :].rearrange("p t q j -> p q j t"),
                     raw[:, :, 4 * q0 : 4 * q0 + 2 * P].rearrange("p j (q t) -> p q j t", t=4),
                 )
-            w_c[m, h, a] = keep.tile([P, HALF], U32, name="w_c%d%d%d" % (m, h, a), align_bytes=64)
-            w_s[m, h, a] = keep.tile([P, HALF], U8, name="w_s%d%d%d" % (m, h, a), align_bytes=64)
+            w_c[m, g, a] = keep.tile([P, HALF], U32, name="w_c%d%d%d" % (m, g, a), align_bytes=64)
+            w_s[m, g, a] = keep.tile([P, HALF], U8, name="w_s%d%d%d" % (m, g, a), align_bytes=64)
             nc.vector.quantize_mx(
-                out=w_c[m, h, a][:].bitcast(FP8X4),
-                scales=w_s[m, h, a][:],
+                out=w_c[m, g, a][:].bitcast(FP8X4),
+                scales=w_s[m, g, a][:],
                 in_=grouped[:].rearrange("p t q j -> p (t q j)"),
             )
 
+        tab_w = table_tile()
+        load_words(tab_w, tab_words, 0)
+        load_words(tab_w, tab_words, 1)
         raws = [load_weight(0, 0)]
         idx1 = load_list(offs, "idx1")
-        tab_w = [table_tile(a) for a in range(PASSES)]
-        load_words(tab_w[0], tab_words, 0)
         load_plane(nc.sync, tab_plane, tab_scales)
-        raws.append(load_weight(1, 0))
-        load_words(tab_w[1], tab_words, 1)
-        raws.append(load_weight(2, 0))
-        raws.append(load_weight(3, 0))
-        v_c, v_s = gather(tab_w, tab_plane, idx1, "v")
+        raws.extend(load_weight(k, 0) for k in range(1, 4))
+        w3_raw.append(load_w3(1))
+        load_dealt(wg2_sb, wg2, 3, 4)
+        v_c, v_s = gather(tab_w, tab_plane, idx1, "v", S)
         for k in range(4):
             quantise_weight(k, 0, raws[k])
-        for s in range(SLICES // 2, SLICES):
+        deal_w3(1, w3_raw[1])
+        for s in range(EARLY, SLICES):
             thermal(s)
         wg1_sb = keep.tile([P, 4, S], F32)
         idx3 = load_list(offs3, "idx3")
@@ -220,7 +226,7 @@ def tile_list_mineral_outcrop_score_kernel(
         def shortwave(s):
             h, c0 = divmod(s * P, HALF)
             cols = slice(c0, c0 + P)
-            b_acc = bank("b%d" % (s % 2), [P, S])
+            b_acc = bank("a%d" % (s % 2), [P, S])
             for a in range(PASSES):
                 nc.tensor.matmul_mx(
                     out=b_acc[:],
@@ -231,7 +237,7 @@ def tile_list_mineral_outcrop_score_kernel(
                     start=(a == 0),
                     stop=(a == PASSES - 1),
                 )
-            d_acc = bank("d%d" % (s % 2), [P, 4, P])
+            d_acc = bank("b%d" % (s % 2), [P, 4, P])
             for j in range(4):
                 for a in range(PASSES):
                     nc.tensor.matmul_mx(
@@ -249,134 +255,91 @@ def tile_list_mineral_outcrop_score_kernel(
             nc.scalar.activation(shifted[:], b_acc[:], ACT.Copy, bias=ROUNDER, scale=1.0 / TWO_PI)
             nc.scalar.activation(turns[:], b_acc[:], ACT.Copy, scale=1.0 / TWO_PI)
             nc.scalar.activation(whole[:], shifted[:], ACT.Copy, bias=ROUNDER, scale=-1.0)
-            both = ring.tile([P, 2, S], F32, name="both", tag="x%d" % (s % 2))
+            both = ring.tile([P, 2, S], F32, name="both", tag="both", bufs=2)
             nc.scalar.activation(both[:, 0, :], d_acc[:].rearrange("p j r -> p (j r)"), ACT.Tanh)
-            r_acc = bank("r%d" % (s % 2), [P, 4, P])
+            r_acc = bank("a%d" % (s % 2 + (2 if s >= 4 else 0)), [P, 4, P])
             for j in range(4):
                 add_transposed(r_acc[:, j, :], turns[:, j * P : (j + 1) * P], whole[:, j * P : (j + 1) * P])
             nc.scalar.activation(both[:, 1, :], r_acc[:].rearrange("p j r -> p (j r)"), ACT.Sin, scale=TWO_PI)
-            h_acc = bank("h%d" % (s % 2), [P, S])
+            h_acc = bank("b%d" % (s % 2 + (2 if s >= 4 else 0)), [P, S])
             for j in range(4):
                 add_transposed(h_acc[:, j * P : (j + 1) * P], both[:, 0, j * P : (j + 1) * P], both[:, 1, j * P : (j + 1) * P])
             h1[s] = ring.tile([P, S], F32, name="feat", tag="feat", bufs=6)
             nc.scalar.activation(h1[s][:], h_acc[:], ACT.Copy, scale=gain_sb[:, s // 4, s % 4 : s % 4 + 1])
 
         w4_w = keep.tile([P, PASSES, 2 * N], U8, align_bytes=64)
-        z_t, z_c, z_s = {}, {}, {}
+        z_c, z_s, score_acc = {}, {}, {}
+        score_banks = ["ab"[i % 2] + "%d" % (i // 2) for i in range(8)]
+        stage_tags = ("turns", "whole", "feat", "feat")
 
-        def quantise_z(g, c, z_in):
-            z_c[g, c] = keep.tile([P, CHUNK], U32, name="z_c%d%d" % (g, c), align_bytes=64)
-            z_s[g, c] = keep.tile([P, CHUNK], U8, name="z_s%d%d" % (g, c), align_bytes=64)
-            nc.vector.quantize_mx(out=z_c[g, c][:].bitcast(FP8X4), scales=z_s[g, c][:], in_=z_in[:])
-
-        def z_tile():
-            return ring.tile([P, 4 * CHUNK], BF16, name="z_in", tag="z_in", bufs=2, align_bytes=64)
-
-        def sum_pair(u):
-            for c in range(CHUNKS):
-                if u == 0:
-                    z_t[c] = ring.tile([P, 2, 2, P, 2], BF16, name="z_t", tag="z_t%d" % c, align_bytes=64)
-                z_acc = bank("z%d" % (c % 2), [P, 2, 2, P])
-                for a in range(2):
-                    cols = slice(c * CHUNK + a * P, c * CHUNK + (a + 1) * P)
-                    for e in range(2):
-                        add_transposed(z_acc[:, a, e, :], lower[2 * u + e][:, cols], upper[2 * u + e][:, cols])
-                nc.scalar.copy(z_t[c][:, :, u, :, :], z_acc[:].rearrange("m a e p -> m a p e"))
-                if u == 1:
-                    words = z_t[c][:].rearrange("m a u p e -> m (a u p e)").bitcast(F32)
-                    w_acc = bank("w%d" % (c % 2), [P, 2, 2, P])
-                    for a in range(2):
-                        for v in range(2):
-                            nc.tensor.transpose(w_acc[:, a, v, :], words[:, (2 * a + v) * P : (2 * a + v + 1) * P], ident[:])
-                    z_in = z_tile()
-                    nc.scalar.copy(
-                        z_in[:].bitcast(F32).rearrange("p (a m u) -> p a m u", a=2, u=2),
-                        w_acc[:].rearrange("p a u m -> p a m u"),
-                    )
-                    quantise_z(0, c, z_in)
-
-        score_acc = {}
-
-        def scores_pass(g, c, half):
+        def scores_pass(g, m0, width, first):
+            tiles = HALF // width
+            z0 = m0 if g == 1 else m0 // HALF * HALF
             if g == 0:
-                score_acc[c, half] = bank("brdh"[c] + "%d" % half, [P, 2, CHUNK])
-            for i in range(2):
-                n0 = (2 * half + i) * P
+                score_acc[m0, first] = bank(score_banks.pop(0), [P, tiles, width])
+            for i in range(tiles):
+                n0 = (first + i) * P
                 nc.tensor.matmul_mx(
-                    out=score_acc[c, half][:, i, :],
+                    out=score_acc[m0, first][:, i, :],
                     lhsT=w4_w[:, g, 2 * n0 : 2 * (n0 + P)].bitcast(FP4X4),
                     lhsT_scale=w4_plane[:, g, n0 : n0 + P],
-                    rhs=z_c[g, c][:].bitcast(FP8X4),
-                    rhs_scale=z_s[g, c][:],
+                    rhs=z_c[g, z0][:, m0 - z0 : m0 - z0 + width].bitcast(FP8X4),
+                    rhs_scale=z_s[g, z0][:, m0 - z0 : m0 - z0 + width],
                     start=(g == 0 and i == 0),
-                    stop=(g == PASSES - 1 and i == 1),
+                    stop=(g == PASSES - 1 and i == tiles - 1),
                 )
 
-        def scores(c):
-            for half in range(2):
-                scores_pass(1, c, half)
-                acc = score_acc[c, half]
-                staged = ring.tile([P, 2, CHUNK], F32, name="staged", tag=("turns", "whole")[half], bufs=2)
-                if half == 0 and c == CHUNKS - 1:
-                    nc.vector.tensor_copy(staged[:], acc[:])
+        def scores(m0, width):
+            tiles = HALF // width
+            for first in range(0, 4, tiles):
+                scores_pass(1, m0, width, first)
+                place_in_ring = len(score_acc) % 4
+                staged = ring.tile([P, tiles, width], F32, name="staged", tag=stage_tags[place_in_ring], bufs=6 if place_in_ring > 1 else 2)
+                if m0 + width == T2:
+                    nc.vector.tensor_copy(staged[:], score_acc.pop((m0, first))[:])
                 else:
-                    nc.scalar.copy(staged[:], acc[:])
-                rows = out[2 * half * P : 2 * (half + 1) * P, c * CHUNK : (c + 1) * CHUNK]
+                    nc.scalar.copy(staged[:], score_acc.pop((m0, first))[:])
+                rows = out[first * P : (first + tiles) * P, m0 : m0 + width]
                 nc.sync.dma_start(rows.rearrange("(i p) m -> p i m", p=P), staged[:])
 
-        lower, upper, lower4, upper4 = {}, {}, {}, {}
-
-        def wide_tile(on_table, k):
-            if on_table:
-                return ring.tile([P, 4, HALF], F32, name="wide", tag="table%d" % k, align_bytes=64)
-            return raw_tile([P, 4, HALF], F32)
+        lower4, upper4 = {}, {}
 
         def place(s):
             g, t = divmod(s, 4)
             page = pa[s % 2]
             nc.vector.tensor_tensor(page[:].indirect(idx3[:]), h1[s][:], wg1_sb[:, t, :], ALU.mult)
-            if g < 0:
-                upper[s] = ring.tile([P, T2], F32, name="upper", tag="upper", bufs=3)
-                nc.vector.tensor_tensor(upper[s][:], pb[s][:], lib_sb[s][:], ALU.max)
-                lower[s] = ring.tile([P, T2], F32, name="lower", tag="x%d" % ((s + LAG) % 2))
-                nc.vector.tensor_tensor(lower[s][:], page[:], lib_sb[s][:], ALU.min)
-                if t % 2 == 1:
-                    sum_pair(t // 2)
-                return
-            for k in range(2):
-                cols = slice(k * HALF, (k + 1) * HALF)
-                if t == 0:
-                    upper4[k] = wide_tile(True, k)
-                nc.vector.tensor_tensor(upper4[k][:, t, :], pb[s][:, cols], lib_sb[s][:, cols], ALU.max)
-            for k in range(2):
-                cols = slice(k * HALF, (k + 1) * HALF)
-                if t == 0:
-                    lower4[k] = wide_tile(False, k)
-                nc.vector.tensor_tensor(lower4[k][:, t, :], page[:, cols], lib_sb[s][:, cols], ALU.min)
+            if t == 0:
+                upper4[g] = ring.tile([P, 4, T2], F32, name="upper4", tag="table", align_bytes=64)
+                lower4[g] = ring.tile([P, 4, T2], F32, name="lower4", tag="raw", bufs=2, align_bytes=64)
+            nc.vector.tensor_tensor(upper4[g][:, t, :], pb[s][:], lib_sb[s][:], ALU.max)
+            nc.vector.tensor_tensor(lower4[g][:, t, :], page[:], lib_sb[s][:], ALU.min)
             if t == 3:
-                for c in range(CHUNKS):
-                    k, m0 = divmod(c * CHUNK, HALF)
-                    z_in = z_tile()
+                for m0, width in PIECES if g == 1 else [(0, HALF), (HALF, HALF)]:
+                    z_in = ring.tile([P, 4 * width], BF16, name="z_in", tag="z_in", bufs=2, align_bytes=64)
                     nc.vector.tensor_tensor(
                         z_in[:].rearrange("p (c i t) -> p c t i", t=4, i=4),
-                        lower4[k][:, :, m0 : m0 + CHUNK].rearrange("p t (c i) -> p c t i", i=4),
-                        upper4[k][:, :, m0 : m0 + CHUNK].rearrange("p t (c i) -> p c t i", i=4),
+                        lower4[g][:, :, m0 : m0 + width].rearrange("p t (c i) -> p c t i", i=4),
+                        upper4[g][:, :, m0 : m0 + width].rearrange("p t (c i) -> p c t i", i=4),
                         ALU.add,
                     )
-                    quantise_z(g, c, z_in)
+                    z_c[g, m0] = keep.tile([P, width], U32, name="z_c%d_%d" % (g, m0), align_bytes=64)
+                    z_s[g, m0] = keep.tile([P, width], U8, name="z_s%d_%d" % (g, m0), align_bytes=64)
+                    nc.vector.quantize_mx(out=z_c[g, m0][:].bitcast(FP8X4), scales=z_s[g, m0][:], in_=z_in[:])
                     if g == PASSES - 1:
-                        scores(c)
+                        scores(m0, width)
 
         for s in range(SLICES + LAG):
+            if s == 0:
+                load_dealt(wg1_sb, wg1, 0, 4)
             if s < 4:
                 load_lib(s)
-            if s == 2:
-                load_wg(nc.sync, wg1_sb, wg1, 0, 4)
             if s < SLICES:
                 shortwave(s)
-            if s < 2:
-                for k in (2 * s, 2 * s + 1):
-                    quantise_weight(k, 1, load_weight(k, 1))
+            if s == 0:
+                raws = [load_weight(k, 1) for k in range(4)]
+            for k in range(4):
+                if s == [0,0,1,1][k]:
+                    quantise_weight(k, 1, raws[k])
             if s == 3:
                 nc.sync.dma_start(w4_w[:].bitcast(I32), w4_words.rearrange("a p c -> p a c").bitcast(I32))
                 for q in range(4):
@@ -385,9 +348,9 @@ def tile_list_mineral_outcrop_score_kernel(
                         w4_scales[:, 4 * q : 4 * q + 4, :].rearrange("a r n -> r a n").bitcast(I32),
                     )
             if s == SLICES - 1:
-                for c in range(CHUNKS):
-                    for half in range(2):
-                        scores_pass(0, c, half)
+                for m0, width in PIECES:
+                    for first in range(0, 4, HALF // width):
+                        scores_pass(0, m0, width, first)
             if s >= LAG:
                 place(s - LAG)
                 if s - LAG + 4 < SLICES:

@@ -20,11 +20,14 @@ ACT = mybir.ActivationFunctionType
 
 P = 128
 PASSES = 2
+GROUP = 512
 SLICES = H // P
-HALF = 512
+BANK = 512
 PIECES = [(0, 256), (256, 256), (512, 256), (768, 128), (896, 128)]
-LAG = 2
 EARLY = 3
+AHEAD = 2
+FEATURE_TILES = 4
+LIB_TILES = 5
 ROUNDER = 1.5 * 2.0**23
 TWO_PI = 2.0 * math.pi
 
@@ -40,182 +43,199 @@ def tile_list_mineral_outcrop_score_kernel(
         ring = ctx.enter_context(tc.tile_pool(name="ring", bufs=1))
         psum = ctx.enter_context(tc.psum_pool(name="psum", bufs=1))
 
+        def bank(tag, shape):
+            return psum.tile(shape, F32, name=tag, tag=tag)
+
         def load_list(source, name):
             tile = lists.tile([P, S // 16], U16, name=name)
             nc.sync.dma_start(tile[:], source)
             return tile
 
-        def bank(tag, shape):
-            return psum.tile(shape, F32, name=tag, tag=tag)
-
-        def load_plane(queue, plane, scales):
-            for q in range(4):
-                queue.dma_start(
-                    plane[32 * q : 32 * q + 4 * PASSES, :].bitcast(I32),
-                    scales[:, 4 * q : 4 * q + 4, :].bitcast(I32),
+        def load_plane(plane, scales):
+            for c in range(4):
+                nc.sync.dma_start(
+                    plane[32 * c : 32 * c + 4 * PASSES, :].bitcast(I32),
+                    scales[:, 4 * c : 4 * c + 4, :].bitcast(I32),
                 )
 
         def load_words(tile, words, a):
             nc.sync.dma_start(tile[:, a, :].bitcast(I32), words[a].rearrange("p t i -> p (t i)").bitcast(I32))
-
-        def load_dealt(tile, wg, t0, t1):
-            rows = wg.rearrange("(q t) j -> q (t j)", t=4)[:, t0 * S : t1 * S]
-            for q in range(4):
-                nc.sync.dma_start(tile[32 * q : 32 * (q + 1), t0:t1, :].rearrange("p t j -> p (t j)"), rows)
 
         tab2_plane = keep.tile([P, T], U8, align_bytes=64)
         w3_plane = keep.tile([P, H], U8, align_bytes=64)
         tab_plane = keep.tile([P, T], U8, align_bytes=64)
         w4_plane = keep.tile([P, PASSES, N], U8, align_bytes=64)
         pb = [keep.tile([P, T2], F32, name="pb%d" % s) for s in range(SLICES)]
-        pa = [keep.tile([P, T2], F32, name="pa%d" % s) for s in range(2)]
-        nc.vector.memset(w3_plane[:].bitcast(I32), 0)
         nc.vector.memset(tab2_plane[:].bitcast(I32), 0)
-        ident = keep.tile([P, P], F32)
-        make_identity(nc, ident[:])
-        nc.gpsimd.memset(w4_plane[:].bitcast(I32), 0)
-        nc.vector.memset(tab_plane[:].bitcast(I32), 0)
-        for s in range(3):
-            nc.vector.memset(pb[s][:].bitcast(I32), 0)
+        nc.vector.memset(w3_plane[:].bitcast(I32), 0)
         warm = keep.tile([P, 16], F32)
         nc.vector.memset(warm[:, 0:1], 0.0)
         nc.scalar.activation(warm[:, 8:9], warm[:, 0:1], ACT.Silu)
+        ident = keep.tile([P, P], F32)
+        make_identity(nc, ident[:])
+        nc.vector.memset(tab_plane[:].bitcast(I32), 0)
+        for page in pb:
+            nc.vector.memset(page[:].bitcast(I32), 0)
+        nc.vector.memset(w4_plane[:].bitcast(I32), 0)
 
-        def table_tile():
-            return ring.tile([P, PASSES, T], U32, name="table", tag="table", align_bytes=64)
+        pa = {}
 
-        def raw_tile():
-            return ring.tile([P, 2, 4, HALF], F32, name="raw", tag="raw", bufs=2, align_bytes=64)
+        def clear_pa(g):
+            pa[g] = ring.tile([P, T2], F32, name="pa", tag="page%d" % g)
+            nc.vector.memset(pa[g][:].bitcast(I32), 0)
 
-        w3_c, w3_s = {}, {}
+        w3_codes, w3_bytes = {}, {}
 
         def load_w3(g):
-            raw = ring.tile([P, PASSES, HALF], I32, name="w3_raw", tag=("grouped0", "lib_sb")[g], bufs=(1, 4)[g], align_bytes=(64, None)[g])
-            words = w3_words.rearrange("a p c i -> p a (c i)")[:, :, 4 * HALF * g : 4 * HALF * (g + 1)]
-            nc.sync.dma_start(raw[:], words.bitcast(I32))
-            return raw
+            loaded = ring.tile([P, PASSES, GROUP], I32, name="w3_loaded", tag="page%d" % g)
+            words = w3_words.rearrange("a p c i -> p a (c i)")[:, :, 4 * GROUP * g : 4 * GROUP * (g + 1)]
+            nc.sync.dma_start(loaded[:], words.bitcast(I32))
+            return loaded
 
-        def deal_w3(g, raw):
-            w3_c[g] = keep.tile([P, PASSES, HALF], I32, name="w3_c%d" % g, align_bytes=64)
-            w3_s[g] = keep.tile([P, HALF], U8, name="w3_s%d" % g, align_bytes=64)
+        def deal_w3(g, loaded):
+            w3_codes[g] = ring.tile([P, PASSES, GROUP], I32, name="w3_codes", tag="lib", bufs=LIB_TILES, align_bytes=64)
+            w3_bytes[g] = keep.tile([P, GROUP], U8, name="w3_bytes%d" % g, align_bytes=64)
             nc.vector.tensor_copy(
-                w3_c[g][:].rearrange("p a (t c i) -> p a c t i", t=4, i=4),
-                raw[:].rearrange("p a (c i t) -> p a c t i", t=4, i=4),
+                w3_codes[g][:].rearrange("p a (t c i) -> p a c t i", t=4, i=4),
+                loaded[:].rearrange("p a (c i t) -> p a c t i", t=4, i=4),
             )
             nc.vector.tensor_copy(
-                w3_s[g][:].rearrange("p (t q) -> p t q", t=4),
-                w3_plane[:, HALF * g : HALF * (g + 1)].rearrange("p (q t) -> p t q", t=4),
+                w3_bytes[g][:].rearrange("p (t q) -> p t q", t=4),
+                w3_plane[:, GROUP * g : GROUP * (g + 1)].rearrange("p (q t) -> p t q", t=4),
             )
 
-        load_plane(nc.gpsimd, w3_plane, w3_scales)
-        tab2_w = table_tile()
+        wg2_rows = ring.tile([P, S], F32, name="wg2_rows", tag="both", bufs=2)
+        nc.sync.dma_start(wg2_rows[:], wg2)
+        tab2_w = ring.tile([P, PASSES, T], U32, name="tab2_w", tag="table", align_bytes=64)
         load_words(tab2_w, tab2_words, 0)
         idx2 = load_list(offs2, "idx2")
-        load_plane(nc.sync, tab2_plane, tab2_scales)
-        w3_raw = [load_w3(0)]
+        load_plane(tab2_plane, tab2_scales)
+        w3_loaded = load_w3(0)
         load_words(tab2_w, tab2_words, 1)
-
-        wg2_sb = keep.tile([P, 4, S], F32)
+        load_plane(w3_plane, w3_scales)
         idx4 = load_list(offs4, "idx4")
-        load_dealt(wg2_sb, wg2, 0, 1)
-        load_dealt(wg2_sb, wg2, 1, 3)
-        for s in range(3, SLICES):
-            nc.gpsimd.memset(pb[s][:].bitcast(I32), 0)
-        gain_sb = keep.tile([P, 2, 4], F32)
-        nc.gpsimd.dma_start(gain_sb[:], gain.rearrange("(g q t) -> q g t", g=2, t=4))
-        for page in pa:
-            nc.gpsimd.memset(page[:].bitcast(I32), 0)
-        deal_w3(0, w3_raw[0])
 
-        def gather(words, plane, idx, name, step):
-            codes = [keep.tile([P, S], U32, name="%s_c%d" % (name, a), align_bytes=64) for a in range(PASSES)]
-            scales = keep.tile([P, S], U8, name=name + "_s", align_bytes=64)
+        wg2_dealt = keep.tile([P, 4, S], F32)
+        turned = bank("a2", [P, 4, P])
+        for j in range(4):
+            nc.tensor.transpose(turned[:, j, :], wg2_rows[:, j * P : (j + 1) * P], ident[:])
+        for t in range(4):
+            spread = ring.tile([P, 4, 4, 32], F32, name="spread", tag=("turns", "whole")[t % 2], bufs=2)
+            every_fourth = turned[:].rearrange("x j (q t) -> x j t q", t=4)[:, :, t : t + 1, :]
+            nc.scalar.copy(spread[:], every_fourth.to_broadcast([P, 4, 4, 32]))
+            back = bank(("b2", "a3")[t % 2], [P, S])
+            for j in range(4):
+                nc.tensor.transpose(back[:, j * P : (j + 1) * P], spread[:, j].rearrange("x c q -> x (c q)"), ident[:])
+            nc.scalar.copy(wg2_dealt[:, t, :], back[:])
+
+        def gather_first(words, plane, idx, tags):
+            codes = [ring.tile([P, S], U32, name="codes", tag=tags[1 + a], align_bytes=64) for a in range(PASSES)]
+            scale_bytes = ring.tile([P, S], U8, name="scale_bytes", tag=tags[0], align_bytes=64)
             nc.vector.tensor_copy(codes[0][:], words[:, 0, :].indirect(idx[:]))
-            nc.vector.tensor_copy(scales[:], plane[:].indirect(idx[:]))
-            for j0 in range(0, S, step):
-                nc.vector.tensor_copy(codes[1][:, j0 : j0 + step], words[:, 1, :].indirect(idx[:, j0 // 16 : (j0 + step) // 16]))
-            return codes, scales
+            nc.vector.tensor_copy(scale_bytes[:], plane[:].indirect(idx[:]))
+            return codes, scale_bytes
 
-        v2_c, v2_s = gather(tab2_w, tab2_plane, idx2, "v2", S // 2)
+        def gather_second(codes, words, idx, step):
+            for j0 in range(0, S, step):
+                offsets = idx[:, j0 // 16 : (j0 + step) // 16]
+                nc.vector.tensor_copy(codes[1][:, j0 : j0 + step], words[:, 1, :].indirect(offsets))
+
+        v2_codes, v2_bytes = gather_first(tab2_w, tab2_plane, idx2, ("v2_bytes", "v2_codes0", "v2_codes1"))
+        deal_w3(0, w3_loaded)
+        gather_second(v2_codes, tab2_w, idx2, S // 2)
+        clear_pa(0)
 
         def thermal(s):
-            g, c0 = divmod(s * P, HALF)
-            if s == EARLY:
-                h2 = ring.tile([P, S], F32, name="feat", tag="grouped2", align_bytes=64)
+            g, t = divmod(s, 4)
+            cols = slice(t * P, (t + 1) * P)
+            if s < EARLY:
+                h2 = ring.tile([P, S], F32, name="h2", tag="early%d" % s, align_bytes=64)
+            elif s == EARLY:
+                h2 = ring.tile([P, S], F32, name="h2", tag="rounded2", align_bytes=64)
             else:
-                h2 = ring.tile([P, S], F32, name="feat", tag="feat", bufs=6)
-            step = S // 2 if s == 0 else S
-            for j0 in range(0, S, step):
+                h2 = ring.tile([P, S], F32, name="h2", tag="features", bufs=FEATURE_TILES)
+            banks = ("a0", "b0") if s == 0 else ("a1",) if s == 1 else ("b1",)
+            step = S // len(banks)
+            for tag, j0 in zip(banks, range(0, S, step)):
                 picked = slice(j0, j0 + step)
-                acc = bank("ab"[(s + j0 // step) % 2] + "0" if s < EARLY else "b1", [P, step])
+                acc = bank(tag, [P, step])
                 for a in range(PASSES):
                     nc.tensor.matmul_mx(
                         out=acc[:],
-                        lhsT=w3_c[g][:, a, c0 : c0 + P].bitcast(FP8X4),
-                        lhsT_scale=w3_s[g][4 * a :, c0 : c0 + P],
-                        rhs=v2_c[a][:, picked].bitcast(FP8X4),
-                        rhs_scale=v2_s[4 * a :, picked],
+                        lhsT=w3_codes[g][:, a, cols].bitcast(FP8X4),
+                        lhsT_scale=w3_bytes[g][4 * a :, cols],
+                        rhs=v2_codes[a][:, picked].bitcast(FP8X4),
+                        rhs_scale=v2_bytes[4 * a :, picked],
                         start=(a == 0),
                         stop=(a == PASSES - 1),
                     )
                 nc.scalar.activation(h2[:, picked], acc[:], ACT.Abs)
                 offsets = idx4[:, j0 // 16 : (j0 + step) // 16]
-                nc.vector.tensor_tensor(pb[s][:].indirect(offsets), h2[:, picked], wg2_sb[:, s % 4, picked], ALU.mult)
+                nc.vector.tensor_tensor(pb[s][:].indirect(offsets), h2[:, picked], wg2_dealt[:, t, picked], ALU.mult)
 
         for s in range(EARLY):
             thermal(s)
 
-        w_c, w_s, raw_pair = {}, {}, {}
-        order = [(1, 0), (0, 0), (1, 1), (0, 1)]
+        weight_order = [("w2", 0), ("w1", 0), ("w2", 1), ("w1", 1)]
+        w_codes, w_bytes = {}, {}
 
-        def load_weight(k, g):
-            m, a = order[k]
-            if k % 2 == 0:
-                raw_pair[g, k // 2] = raw_tile()
-            raw = raw_pair[g, k // 2][:, k % 2]
-            rows = (w1, w2)[m][512 * a : 512 * (a + 1), HALF * g : HALF * (g + 1)]
-            nc.sync.dma_start(raw, rows.rearrange("(p j) c -> p j c", j=4))
-            return raw
+        def load_weights(g):
+            loaded = []
+            for n, (name, a) in enumerate(weight_order):
+                if n % 2 == 0:
+                    pair = ring.tile([P, 2, 4, GROUP], F32, name="pair", tag="rows", bufs=2, align_bytes=64)
+                rows = {"w1": w1, "w2": w2}[name][GROUP * a : GROUP * (a + 1), GROUP * g : GROUP * (g + 1)]
+                nc.sync.dma_start(pair[:, n % 2], rows.rearrange("(p i) c -> p i c", i=4))
+                loaded.append(pair[:, n % 2])
+            return loaded
 
-        def quantise_weight(k, g, raw):
-            m, a = order[k]
-            grouped = ring.tile([P, 4, P, 4], BF16, name="grouped", tag="grouped%d" % k, align_bytes=64)
-            for q0 in range(0, P, P // 2):
+        def quantise_weight(n, g, loaded):
+            rounded = ring.tile([P, 4, P, 4], BF16, name="rounded", tag="rounded%d" % n, align_bytes=64)
+            for t0 in (0, 2):
                 nc.scalar.copy(
-                    grouped[:, :, q0 : q0 + P // 2, :].rearrange("p t q j -> p q j t"),
-                    raw[:, :, 4 * q0 : 4 * q0 + 2 * P].rearrange("p j (q t) -> p q j t", t=4),
+                    rounded[:, t0 : t0 + 2].rearrange("p t q i -> p q i t"),
+                    loaded.rearrange("p i (q t) -> p q i t", t=4)[:, :, :, t0 : t0 + 2],
                 )
-            w_c[m, g, a] = keep.tile([P, HALF], U32, name="w_c%d%d%d" % (m, g, a), align_bytes=64)
-            w_s[m, g, a] = keep.tile([P, HALF], U8, name="w_s%d%d%d" % (m, g, a), align_bytes=64)
+            key = weight_order[n] + (g,)
+            w_codes[key] = keep.tile([P, GROUP], U32, name="%s_codes%d%d" % key, align_bytes=64)
+            w_bytes[key] = keep.tile([P, GROUP], U8, name="%s_bytes%d%d" % key, align_bytes=64)
             nc.vector.quantize_mx(
-                out=w_c[m, g, a][:].bitcast(FP8X4),
-                scales=w_s[m, g, a][:],
-                in_=grouped[:].rearrange("p t q j -> p (t q j)"),
+                out=w_codes[key][:].bitcast(FP8X4),
+                scales=w_bytes[key][:],
+                in_=rounded[:].rearrange("p t q i -> p (t q i)"),
             )
 
-        tab_w = table_tile()
+        tab_w = keep.tile([P, PASSES, T], U32, align_bytes=64)
         load_words(tab_w, tab_words, 0)
         load_words(tab_w, tab_words, 1)
-        raws = [load_weight(0, 0)]
         idx1 = load_list(offs, "idx1")
-        load_plane(nc.sync, tab_plane, tab_scales)
-        raws.extend(load_weight(k, 0) for k in range(1, 4))
-        w3_raw.append(load_w3(1))
-        load_dealt(wg2_sb, wg2, 3, 4)
-        v_c, v_s = gather(tab_w, tab_plane, idx1, "v", S)
-        for k in range(4):
-            quantise_weight(k, 0, raws[k])
-        deal_w3(1, w3_raw[1])
+        load_plane(tab_plane, tab_scales)
+        w_loaded = load_weights(0)
+        w3_loaded = load_w3(1)
+        v_codes, v_bytes = gather_first(tab_w, tab_plane, idx1, ("early0", "early1", "early2"))
+        gather_second(v_codes, tab_w, idx1, S)
+        for n in range(4):
+            quantise_weight(n, 0, w_loaded[n])
+        deal_w3(1, w3_loaded)
+        clear_pa(1)
         for s in range(EARLY, SLICES):
             thermal(s)
-        wg1_sb = keep.tile([P, 4, S], F32)
-        idx3 = load_list(offs3, "idx3")
 
-        lib_sb = {}
+        idx3 = load_list(offs3, "idx3")
+        gain_dealt = keep.tile([P, 2, 4], F32)
+        nc.sync.dma_start(gain_dealt[:], gain.rearrange("(g p t) -> p g t", g=2, t=4))
+        wg1_dealt = keep.tile([P, 4, S], F32)
+        for c in range(4):
+            nc.sync.dma_start(
+                wg1_dealt[32 * c : 32 * (c + 1)].rearrange("p t j -> p (t j)"),
+                wg1.rearrange("(q t) j -> q (t j)", t=4),
+            )
+
+        lib_rows = {}
 
         def load_lib(s):
-            lib_sb[s] = ring.tile([P, T2], F32, name="lib_sb", tag="lib_sb", bufs=4)
-            nc.sync.dma_start(lib_sb[s][:], lib.rearrange("(g q t) m -> g t q m", g=2, t=4)[s // 4, s % 4])
+            lib_rows[s] = ring.tile([P, T2], F32, name="lib_rows", tag="lib", bufs=LIB_TILES, align_bytes=64)
+            nc.sync.dma_start(lib_rows[s][:], lib.rearrange("(g p t) m -> g t p m", g=2, t=4)[s // 4, s % 4])
 
         def add_transposed(dst, first, second):
             nc.tensor.matmul(dst, lhsT=first, rhs=ident[:], start=True, stop=False, is_transpose=True)
@@ -224,16 +244,16 @@ def tile_list_mineral_outcrop_score_kernel(
         h1 = {}
 
         def shortwave(s):
-            h, c0 = divmod(s * P, HALF)
-            cols = slice(c0, c0 + P)
+            g, t = divmod(s, 4)
+            cols = slice(t * P, (t + 1) * P)
             b_acc = bank("a%d" % (s % 2), [P, S])
             for a in range(PASSES):
                 nc.tensor.matmul_mx(
                     out=b_acc[:],
-                    lhsT=w_c[1, h, a][:, cols].bitcast(FP8X4),
-                    lhsT_scale=w_s[1, h, a][:, cols],
-                    rhs=v_c[a][:].bitcast(FP8X4),
-                    rhs_scale=v_s[4 * a :, :],
+                    lhsT=w_codes["w2", a, g][:, cols].bitcast(FP8X4),
+                    lhsT_scale=w_bytes["w2", a, g][:, cols],
+                    rhs=v_codes[a][:].bitcast(FP8X4),
+                    rhs_scale=v_bytes[4 * a :, :],
                     start=(a == 0),
                     stop=(a == PASSES - 1),
                 )
@@ -242,116 +262,116 @@ def tile_list_mineral_outcrop_score_kernel(
                 for a in range(PASSES):
                     nc.tensor.matmul_mx(
                         out=d_acc[:, j, :],
-                        lhsT=v_c[a][:, j * P : (j + 1) * P].bitcast(FP8X4),
-                        lhsT_scale=v_s[4 * a :, j * P : (j + 1) * P],
-                        rhs=w_c[0, h, a][:, cols].bitcast(FP8X4),
-                        rhs_scale=w_s[0, h, a][:, cols],
+                        lhsT=v_codes[a][:, j * P : (j + 1) * P].bitcast(FP8X4),
+                        lhsT_scale=v_bytes[4 * a :, j * P : (j + 1) * P],
+                        rhs=w_codes["w1", a, g][:, cols].bitcast(FP8X4),
+                        rhs_scale=w_bytes["w1", a, g][:, cols],
                         start=(a == 0),
                         stop=(a == PASSES - 1),
                     )
-            shifted = ring.tile([P, S], U32, name="shifted", tag="shifted", bufs=1)
+            shifted = ring.tile([P, S], U32, name="shifted", tag="shifted")
             turns = ring.tile([P, S], F32, name="turns", tag="turns", bufs=2)
             whole = ring.tile([P, S], F32, name="whole", tag="whole", bufs=2)
             nc.scalar.activation(shifted[:], b_acc[:], ACT.Copy, bias=ROUNDER, scale=1.0 / TWO_PI)
             nc.scalar.activation(turns[:], b_acc[:], ACT.Copy, scale=1.0 / TWO_PI)
             nc.scalar.activation(whole[:], shifted[:], ACT.Copy, bias=ROUNDER, scale=-1.0)
             both = ring.tile([P, 2, S], F32, name="both", tag="both", bufs=2)
-            nc.scalar.activation(both[:, 0, :], d_acc[:].rearrange("p j r -> p (j r)"), ACT.Tanh)
-            r_acc = bank("a%d" % (s % 2 + (2 if s >= 4 else 0)), [P, 4, P])
+            nc.scalar.activation(both[:, 0, :], d_acc[:].rearrange("x j r -> x (j r)"), ACT.Tanh)
+            angle = bank("a%d" % (s % 2 + 2 * g), [P, 4, P])
             for j in range(4):
-                add_transposed(r_acc[:, j, :], turns[:, j * P : (j + 1) * P], whole[:, j * P : (j + 1) * P])
-            nc.scalar.activation(both[:, 1, :], r_acc[:].rearrange("p j r -> p (j r)"), ACT.Sin, scale=TWO_PI)
-            h_acc = bank("b%d" % (s % 2 + (2 if s >= 4 else 0)), [P, S])
+                add_transposed(angle[:, j, :], turns[:, j * P : (j + 1) * P], whole[:, j * P : (j + 1) * P])
+            nc.scalar.activation(both[:, 1, :], angle[:].rearrange("x j r -> x (j r)"), ACT.Sin, scale=TWO_PI)
+            total = bank("b%d" % (s % 2 + 2 * g), [P, S])
             for j in range(4):
-                add_transposed(h_acc[:, j * P : (j + 1) * P], both[:, 0, j * P : (j + 1) * P], both[:, 1, j * P : (j + 1) * P])
-            h1[s] = ring.tile([P, S], F32, name="feat", tag="feat", bufs=6)
-            nc.scalar.activation(h1[s][:], h_acc[:], ACT.Copy, scale=gain_sb[:, s // 4, s % 4 : s % 4 + 1])
+                block = slice(j * P, (j + 1) * P)
+                add_transposed(total[:, block], both[:, 0, block], both[:, 1, block])
+            h1[s] = ring.tile([P, S], F32, name="h1", tag="features", bufs=FEATURE_TILES)
+            nc.scalar.activation(h1[s][:], total[:], ACT.Copy, scale=gain_dealt[:, g, t : t + 1])
 
         w4_w = keep.tile([P, PASSES, 2 * N], U8, align_bytes=64)
-        z_c, z_s, score_acc = {}, {}, {}
-        score_banks = ["ab"[i % 2] + "%d" % (i // 2) for i in range(8)]
-        stage_tags = ("turns", "whole", "feat", "feat")
+        z_codes, z_bytes, score_acc = {}, {}, {}
+        free_banks = ["ab"[n % 2] + "%d" % (n // 2) for n in range(8)]
+        stage_tags = [("turns", 2), ("whole", 2), ("features", FEATURE_TILES), ("features", FEATURE_TILES)]
 
-        def scores_pass(g, m0, width, first):
-            tiles = HALF // width
-            z0 = m0 if g == 1 else m0 // HALF * HALF
+        def score_pass(g, m0, width, first):
+            tiles = BANK // width
             if g == 0:
-                score_acc[m0, first] = bank(score_banks.pop(0), [P, tiles, width])
-            for i in range(tiles):
-                n0 = (first + i) * P
+                score_acc[m0, first] = bank(free_banks.pop(0), [P, tiles, width])
+            for n in range(tiles):
+                n0 = (first + n) * P
                 nc.tensor.matmul_mx(
-                    out=score_acc[m0, first][:, i, :],
+                    out=score_acc[m0, first][:, n, :],
                     lhsT=w4_w[:, g, 2 * n0 : 2 * (n0 + P)].bitcast(FP4X4),
                     lhsT_scale=w4_plane[:, g, n0 : n0 + P],
-                    rhs=z_c[g, z0][:, m0 - z0 : m0 - z0 + width].bitcast(FP8X4),
-                    rhs_scale=z_s[g, z0][:, m0 - z0 : m0 - z0 + width],
-                    start=(g == 0 and i == 0),
-                    stop=(g == PASSES - 1 and i == tiles - 1),
+                    rhs=z_codes[g, m0][:].bitcast(FP8X4),
+                    rhs_scale=z_bytes[g, m0][:],
+                    start=(g == 0 and n == 0),
+                    stop=(g == PASSES - 1 and n == tiles - 1),
                 )
 
-        def scores(m0, width):
-            tiles = HALF // width
-            for first in range(0, 4, tiles):
-                scores_pass(1, m0, width, first)
-                place_in_ring = len(score_acc) % 4
-                staged = ring.tile([P, tiles, width], F32, name="staged", tag=stage_tags[place_in_ring], bufs=6 if place_in_ring > 1 else 2)
+        def finish_scores(m0, width):
+            tiles = BANK // width
+            for first in range(0, N // P, tiles):
+                score_pass(PASSES - 1, m0, width, first)
+                tag, bufs = stage_tags[len(score_acc) % len(stage_tags)]
+                staged = ring.tile([P, tiles, width], F32, name="staged", tag=tag, bufs=bufs)
+                acc = score_acc.pop((m0, first))
                 if m0 + width == T2:
-                    nc.vector.tensor_copy(staged[:], score_acc.pop((m0, first))[:])
+                    nc.vector.tensor_copy(staged[:], acc[:])
                 else:
-                    nc.scalar.copy(staged[:], score_acc.pop((m0, first))[:])
+                    nc.scalar.copy(staged[:], acc[:])
                 rows = out[first * P : (first + tiles) * P, m0 : m0 + width]
-                nc.sync.dma_start(rows.rearrange("(i p) m -> p i m", p=P), staged[:])
+                nc.sync.dma_start(rows.rearrange("(n p) m -> p n m", p=P), staged[:])
 
-        lower4, upper4 = {}, {}
+        lower, upper = {}, {}
 
         def place(s):
             g, t = divmod(s, 4)
             page = pa[s % 2]
-            nc.vector.tensor_tensor(page[:].indirect(idx3[:]), h1[s][:], wg1_sb[:, t, :], ALU.mult)
+            nc.vector.tensor_tensor(page[:].indirect(idx3[:]), h1[s][:], wg1_dealt[:, t, :], ALU.mult)
             if t == 0:
-                upper4[g] = ring.tile([P, 4, T2], F32, name="upper4", tag="table", align_bytes=64)
-                lower4[g] = ring.tile([P, 4, T2], F32, name="lower4", tag="raw", bufs=2, align_bytes=64)
-            nc.vector.tensor_tensor(upper4[g][:, t, :], pb[s][:], lib_sb[s][:], ALU.max)
-            nc.vector.tensor_tensor(lower4[g][:, t, :], page[:], lib_sb[s][:], ALU.min)
-            if t == 3:
-                for m0, width in PIECES if g == 1 else [(0, HALF), (HALF, HALF)]:
-                    z_in = ring.tile([P, 4 * width], BF16, name="z_in", tag="z_in", bufs=2, align_bytes=64)
-                    nc.vector.tensor_tensor(
-                        z_in[:].rearrange("p (c i t) -> p c t i", t=4, i=4),
-                        lower4[g][:, :, m0 : m0 + width].rearrange("p t (c i) -> p c t i", i=4),
-                        upper4[g][:, :, m0 : m0 + width].rearrange("p t (c i) -> p c t i", i=4),
-                        ALU.add,
-                    )
-                    z_c[g, m0] = keep.tile([P, width], U32, name="z_c%d_%d" % (g, m0), align_bytes=64)
-                    z_s[g, m0] = keep.tile([P, width], U8, name="z_s%d_%d" % (g, m0), align_bytes=64)
-                    nc.vector.quantize_mx(out=z_c[g, m0][:].bitcast(FP8X4), scales=z_s[g, m0][:], in_=z_in[:])
-                    if g == PASSES - 1:
-                        scores(m0, width)
+                upper[g] = ring.tile([P, 4, T2], F32, name="upper", tag="table", align_bytes=64)
+                lower[g] = ring.tile([P, 4, T2], F32, name="lower", tag="rows", bufs=2, align_bytes=64)
+            nc.vector.tensor_tensor(upper[g][:, t, :], pb[s][:], lib_rows[s][:], ALU.max)
+            nc.vector.tensor_tensor(lower[g][:, t, :], page[:], lib_rows[s][:], ALU.min)
+            if t < 3:
+                return
+            for m0, width in PIECES:
+                z = ring.tile([P, 4 * width], BF16, name="z", tag="z", bufs=2, align_bytes=64)
+                nc.vector.tensor_tensor(
+                    z[:].rearrange("p (c i t) -> p c t i", t=4, i=4),
+                    lower[g][:, :, m0 : m0 + width].rearrange("p t (c i) -> p c t i", i=4),
+                    upper[g][:, :, m0 : m0 + width].rearrange("p t (c i) -> p c t i", i=4),
+                    ALU.add,
+                )
+                z_codes[g, m0] = keep.tile([P, width], U32, name="z_codes%d_%d" % (g, m0), align_bytes=64)
+                z_bytes[g, m0] = keep.tile([P, width], U8, name="z_bytes%d_%d" % (g, m0), align_bytes=64)
+                nc.vector.quantize_mx(out=z_codes[g, m0][:].bitcast(FP8X4), scales=z_bytes[g, m0][:], in_=z[:])
+                if g == PASSES - 1:
+                    finish_scores(m0, width)
 
-        for s in range(SLICES + LAG):
-            if s == 0:
-                load_dealt(wg1_sb, wg1, 0, 4)
-            if s < 4:
-                load_lib(s)
-            if s < SLICES:
-                shortwave(s)
-            if s == 0:
-                raws = [load_weight(k, 1) for k in range(4)]
-            for k in range(4):
-                if s == [0,0,1,1][k]:
-                    quantise_weight(k, 1, raws[k])
-            if s == 3:
+        for step in range(SLICES + AHEAD):
+            if step < LIB_TILES:
+                load_lib(step)
+            if step < SLICES:
+                shortwave(step)
+            if step == 0:
+                w_loaded = load_weights(1)
+            if step < 2:
+                quantise_weight(2 * step, 1, w_loaded[2 * step])
+                quantise_weight(2 * step + 1, 1, w_loaded[2 * step + 1])
+            if step == 3:
                 nc.sync.dma_start(w4_w[:].bitcast(I32), w4_words.rearrange("a p c -> p a c").bitcast(I32))
-                for q in range(4):
+                for c in range(4):
                     nc.sync.dma_start(
-                        w4_plane[32 * q : 32 * q + 4, :, :].bitcast(I32),
-                        w4_scales[:, 4 * q : 4 * q + 4, :].rearrange("a r n -> r a n").bitcast(I32),
+                        w4_plane[32 * c : 32 * c + 4, :, :].bitcast(I32),
+                        w4_scales[:, 4 * c : 4 * c + 4, :].rearrange("a r n -> r a n").bitcast(I32),
                     )
-            if s == SLICES - 1:
+            if step == SLICES - 1:
                 for m0, width in PIECES:
-                    for first in range(0, 4, HALF // width):
-                        scores_pass(0, m0, width, first)
-            if s >= LAG:
-                place(s - LAG)
-                if s - LAG + 4 < SLICES:
-                    load_lib(s - LAG + 4)
+                    for first in range(0, N // P, BANK // width):
+                        score_pass(0, m0, width, first)
+            if step >= AHEAD:
+                place(step - AHEAD)
+                if step - AHEAD + LIB_TILES < SLICES:
+                    load_lib(step - AHEAD + LIB_TILES)

import math
from contextlib import ExitStack

import concourse.mybir as mybir
from concourse.masks import make_identity

K, T, S, T2, H, N = 1024, 2048, 512, 1024, 1024, 512
FLOPS = 2 * (3 * K * H * S + H * N * T2)

F32 = mybir.dt.float32
BF16 = mybir.dt.bfloat16
I32 = mybir.dt.int32
U32 = mybir.dt.uint32
U16 = mybir.dt.uint16
U8 = mybir.dt.uint8
FP8X4 = mybir.dt.float8_e4m3fn_x4
FP4X4 = mybir.dt.float4_e2m1fn_x4
ALU = mybir.AluOpType
ACT = mybir.ActivationFunctionType

P = 128
PASSES = 2
GROUP = 512
SLICES = H // P
BANK = 512
PIECES = [(0, 256), (256, 256), (512, 256), (768, 128), (896, 128)]
EARLY = 3
AHEAD = 2
FEATURE_TILES = 4
LIB_TILES = 5
ROUNDER = 1.5 * 2.0**23
TWO_PI = 2.0 * math.pi


def tile_list_mineral_outcrop_score_kernel(
    tc, tab_words, tab_scales, tab2_words, tab2_scales, offs, offs2, offs3, offs4,
    w1, w2, gain, w3_words, w3_scales, wg1, wg2, lib, w4_words, w4_scales, out,
):
    nc = tc.nc
    with ExitStack() as ctx:
        lists = ctx.enter_context(tc.tile_pool(name="lists", bufs=1))
        keep = ctx.enter_context(tc.tile_pool(name="keep", bufs=1))
        ring = ctx.enter_context(tc.tile_pool(name="ring", bufs=1))
        psum = ctx.enter_context(tc.psum_pool(name="psum", bufs=1))

        def bank(tag, shape):
            return psum.tile(shape, F32, name=tag, tag=tag)

        def load_list(source, name):
            tile = lists.tile([P, S // 16], U16, name=name)
            nc.sync.dma_start(tile[:], source)
            return tile

        def load_plane(plane, scales):
            for c in range(4):
                nc.sync.dma_start(
                    plane[32 * c : 32 * c + 4 * PASSES, :].bitcast(I32),
                    scales[:, 4 * c : 4 * c + 4, :].bitcast(I32),
                )

        def load_words(tile, words, a):
            nc.sync.dma_start(tile[:, a, :].bitcast(I32), words[a].rearrange("p t i -> p (t i)").bitcast(I32))

        tab2_plane = keep.tile([P, T], U8, align_bytes=64)
        w3_plane = keep.tile([P, H], U8, align_bytes=64)
        tab_plane = keep.tile([P, T], U8, align_bytes=64)
        w4_plane = keep.tile([P, PASSES, N], U8, align_bytes=64)
        pb = [keep.tile([P, T2], F32, name="pb%d" % s) for s in range(SLICES)]
        nc.vector.memset(tab2_plane[:].bitcast(I32), 0)
        nc.vector.memset(w3_plane[:].bitcast(I32), 0)
        warm = keep.tile([P, 16], F32)
        nc.vector.memset(warm[:, 0:1], 0.0)
        nc.scalar.activation(warm[:, 8:9], warm[:, 0:1], ACT.Silu)
        ident = keep.tile([P, P], F32)
        make_identity(nc, ident[:])
        nc.vector.memset(tab_plane[:].bitcast(I32), 0)
        for page in pb:
            nc.vector.memset(page[:].bitcast(I32), 0)
        nc.vector.memset(w4_plane[:].bitcast(I32), 0)

        pa = {}

        def clear_pa(g):
            pa[g] = ring.tile([P, T2], F32, name="pa", tag="page%d" % g)
            nc.vector.memset(pa[g][:].bitcast(I32), 0)

        w3_codes, w3_bytes = {}, {}

        def load_w3(g):
            loaded = ring.tile([P, PASSES, GROUP], I32, name="w3_loaded", tag="page%d" % g)
            words = w3_words.rearrange("a p c i -> p a (c i)")[:, :, 4 * GROUP * g : 4 * GROUP * (g + 1)]
            nc.sync.dma_start(loaded[:], words.bitcast(I32))
            return loaded

        def deal_w3(g, loaded):
            w3_codes[g] = ring.tile([P, PASSES, GROUP], I32, name="w3_codes", tag="lib", bufs=LIB_TILES, align_bytes=64)
            w3_bytes[g] = keep.tile([P, GROUP], U8, name="w3_bytes%d" % g, align_bytes=64)
            nc.vector.tensor_copy(
                w3_codes[g][:].rearrange("p a (t c i) -> p a c t i", t=4, i=4),
                loaded[:].rearrange("p a (c i t) -> p a c t i", t=4, i=4),
            )
            nc.vector.tensor_copy(
                w3_bytes[g][:].rearrange("p (t q) -> p t q", t=4),
                w3_plane[:, GROUP * g : GROUP * (g + 1)].rearrange("p (q t) -> p t q", t=4),
            )

        wg2_rows = ring.tile([P, S], F32, name="wg2_rows", tag="both", bufs=2)
        nc.sync.dma_start(wg2_rows[:], wg2)
        tab2_w = ring.tile([P, PASSES, T], U32, name="tab2_w", tag="table", align_bytes=64)
        load_words(tab2_w, tab2_words, 0)
        idx2 = load_list(offs2, "idx2")
        load_plane(tab2_plane, tab2_scales)
        w3_loaded = load_w3(0)
        load_words(tab2_w, tab2_words, 1)
        load_plane(w3_plane, w3_scales)
        idx4 = load_list(offs4, "idx4")

        wg2_dealt = keep.tile([P, 4, S], F32)
        turned = bank("a2", [P, 4, P])
        for j in range(4):
            nc.tensor.transpose(turned[:, j, :], wg2_rows[:, j * P : (j + 1) * P], ident[:])
        for t in range(4):
            spread = ring.tile([P, 4, 4, 32], F32, name="spread", tag=("turns", "whole")[t % 2], bufs=2)
            every_fourth = turned[:].rearrange("x j (q t) -> x j t q", t=4)[:, :, t : t + 1, :]
            nc.scalar.copy(spread[:], every_fourth.to_broadcast([P, 4, 4, 32]))
            back = bank(("b2", "a3")[t % 2], [P, S])
            for j in range(4):
                nc.tensor.transpose(back[:, j * P : (j + 1) * P], spread[:, j].rearrange("x c q -> x (c q)"), ident[:])
            nc.scalar.copy(wg2_dealt[:, t, :], back[:])

        def gather_first(words, plane, idx, tags):
            codes = [ring.tile([P, S], U32, name="codes", tag=tags[1 + a], align_bytes=64) for a in range(PASSES)]
            scale_bytes = ring.tile([P, S], U8, name="scale_bytes", tag=tags[0], align_bytes=64)
            nc.vector.tensor_copy(codes[0][:], words[:, 0, :].indirect(idx[:]))
            nc.vector.tensor_copy(scale_bytes[:], plane[:].indirect(idx[:]))
            return codes, scale_bytes

        def gather_second(codes, words, idx, step):
            for j0 in range(0, S, step):
                offsets = idx[:, j0 // 16 : (j0 + step) // 16]
                nc.vector.tensor_copy(codes[1][:, j0 : j0 + step], words[:, 1, :].indirect(offsets))

        v2_codes, v2_bytes = gather_first(tab2_w, tab2_plane, idx2, ("v2_bytes", "v2_codes0", "v2_codes1"))
        deal_w3(0, w3_loaded)
        gather_second(v2_codes, tab2_w, idx2, S // 2)
        clear_pa(0)

        def thermal(s):
            g, t = divmod(s, 4)
            cols = slice(t * P, (t + 1) * P)
            if s < EARLY:
                h2 = ring.tile([P, S], F32, name="h2", tag="early%d" % s, align_bytes=64)
            elif s == EARLY:
                h2 = ring.tile([P, S], F32, name="h2", tag="rounded2", align_bytes=64)
            else:
                h2 = ring.tile([P, S], F32, name="h2", tag="features", bufs=FEATURE_TILES)
            banks = ("a0", "b0") if s == 0 else ("a1",) if s == 1 else ("b1",)
            step = S // len(banks)
            for tag, j0 in zip(banks, range(0, S, step)):
                picked = slice(j0, j0 + step)
                acc = bank(tag, [P, step])
                for a in range(PASSES):
                    nc.tensor.matmul_mx(
                        out=acc[:],
                        lhsT=w3_codes[g][:, a, cols].bitcast(FP8X4),
                        lhsT_scale=w3_bytes[g][4 * a :, cols],
                        rhs=v2_codes[a][:, picked].bitcast(FP8X4),
                        rhs_scale=v2_bytes[4 * a :, picked],
                        start=(a == 0),
                        stop=(a == PASSES - 1),
                    )
                nc.scalar.activation(h2[:, picked], acc[:], ACT.Abs)
                offsets = idx4[:, j0 // 16 : (j0 + step) // 16]
                nc.vector.tensor_tensor(pb[s][:].indirect(offsets), h2[:, picked], wg2_dealt[:, t, picked], ALU.mult)

        for s in range(EARLY):
            thermal(s)

        weight_order = [("w2", 0), ("w1", 0), ("w2", 1), ("w1", 1)]
        w_codes, w_bytes = {}, {}

        def load_weights(g):
            loaded = []
            for n, (name, a) in enumerate(weight_order):
                if n % 2 == 0:
                    pair = ring.tile([P, 2, 4, GROUP], F32, name="pair", tag="rows", bufs=2, align_bytes=64)
                rows = {"w1": w1, "w2": w2}[name][GROUP * a : GROUP * (a + 1), GROUP * g : GROUP * (g + 1)]
                nc.sync.dma_start(pair[:, n % 2], rows.rearrange("(p i) c -> p i c", i=4))
                loaded.append(pair[:, n % 2])
            return loaded

        def quantise_weight(n, g, loaded):
            rounded = ring.tile([P, 4, P, 4], BF16, name="rounded", tag="rounded%d" % n, align_bytes=64)
            for t0 in (0, 2):
                nc.scalar.copy(
                    rounded[:, t0 : t0 + 2].rearrange("p t q i -> p q i t"),
                    loaded.rearrange("p i (q t) -> p q i t", t=4)[:, :, :, t0 : t0 + 2],
                )
            key = weight_order[n] + (g,)
            w_codes[key] = keep.tile([P, GROUP], U32, name="%s_codes%d%d" % key, align_bytes=64)
            w_bytes[key] = keep.tile([P, GROUP], U8, name="%s_bytes%d%d" % key, align_bytes=64)
            nc.vector.quantize_mx(
                out=w_codes[key][:].bitcast(FP8X4),
                scales=w_bytes[key][:],
                in_=rounded[:].rearrange("p t q i -> p (t q i)"),
            )

        tab_w = keep.tile([P, PASSES, T], U32, align_bytes=64)
        load_words(tab_w, tab_words, 0)
        load_words(tab_w, tab_words, 1)
        idx1 = load_list(offs, "idx1")
        load_plane(tab_plane, tab_scales)
        w_loaded = load_weights(0)
        w3_loaded = load_w3(1)
        v_codes, v_bytes = gather_first(tab_w, tab_plane, idx1, ("early0", "early1", "early2"))
        gather_second(v_codes, tab_w, idx1, S)
        for n in range(4):
            quantise_weight(n, 0, w_loaded[n])
        deal_w3(1, w3_loaded)
        clear_pa(1)
        for s in range(EARLY, SLICES):
            thermal(s)

        idx3 = load_list(offs3, "idx3")
        gain_dealt = keep.tile([P, 2, 4], F32)
        nc.sync.dma_start(gain_dealt[:], gain.rearrange("(g p t) -> p g t", g=2, t=4))
        wg1_dealt = keep.tile([P, 4, S], F32)
        for c in range(4):
            nc.sync.dma_start(
                wg1_dealt[32 * c : 32 * (c + 1)].rearrange("p t j -> p (t j)"),
                wg1.rearrange("(q t) j -> q (t j)", t=4),
            )

        lib_rows = {}

        def load_lib(s):
            lib_rows[s] = ring.tile([P, T2], F32, name="lib_rows", tag="lib", bufs=LIB_TILES, align_bytes=64)
            nc.sync.dma_start(lib_rows[s][:], lib.rearrange("(g p t) m -> g t p m", g=2, t=4)[s // 4, s % 4])

        def add_transposed(dst, first, second):
            nc.tensor.matmul(dst, lhsT=first, rhs=ident[:], start=True, stop=False, is_transpose=True)
            nc.tensor.matmul(dst, lhsT=second, rhs=ident[:], start=False, stop=True, is_transpose=True)

        h1 = {}

        def shortwave(s):
            g, t = divmod(s, 4)
            cols = slice(t * P, (t + 1) * P)
            b_acc = bank("a%d" % (s % 2), [P, S])
            for a in range(PASSES):
                nc.tensor.matmul_mx(
                    out=b_acc[:],
                    lhsT=w_codes["w2", a, g][:, cols].bitcast(FP8X4),
                    lhsT_scale=w_bytes["w2", a, g][:, cols],
                    rhs=v_codes[a][:].bitcast(FP8X4),
                    rhs_scale=v_bytes[4 * a :, :],
                    start=(a == 0),
                    stop=(a == PASSES - 1),
                )
            d_acc = bank("b%d" % (s % 2), [P, 4, P])
            for j in range(4):
                for a in range(PASSES):
                    nc.tensor.matmul_mx(
                        out=d_acc[:, j, :],
                        lhsT=v_codes[a][:, j * P : (j + 1) * P].bitcast(FP8X4),
                        lhsT_scale=v_bytes[4 * a :, j * P : (j + 1) * P],
                        rhs=w_codes["w1", a, g][:, cols].bitcast(FP8X4),
                        rhs_scale=w_bytes["w1", a, g][:, cols],
                        start=(a == 0),
                        stop=(a == PASSES - 1),
                    )
            shifted = ring.tile([P, S], U32, name="shifted", tag="shifted")
            turns = ring.tile([P, S], F32, name="turns", tag="turns", bufs=2)
            whole = ring.tile([P, S], F32, name="whole", tag="whole", bufs=2)
            nc.scalar.activation(shifted[:], b_acc[:], ACT.Copy, bias=ROUNDER, scale=1.0 / TWO_PI)
            nc.scalar.activation(turns[:], b_acc[:], ACT.Copy, scale=1.0 / TWO_PI)
            nc.scalar.activation(whole[:], shifted[:], ACT.Copy, bias=ROUNDER, scale=-1.0)
            both = ring.tile([P, 2, S], F32, name="both", tag="both", bufs=2)
            nc.scalar.activation(both[:, 0, :], d_acc[:].rearrange("x j r -> x (j r)"), ACT.Tanh)
            angle = bank("a%d" % (s % 2 + 2 * g), [P, 4, P])
            for j in range(4):
                add_transposed(angle[:, j, :], turns[:, j * P : (j + 1) * P], whole[:, j * P : (j + 1) * P])
            nc.scalar.activation(both[:, 1, :], angle[:].rearrange("x j r -> x (j r)"), ACT.Sin, scale=TWO_PI)
            total = bank("b%d" % (s % 2 + 2 * g), [P, S])
            for j in range(4):
                block = slice(j * P, (j + 1) * P)
                add_transposed(total[:, block], both[:, 0, block], both[:, 1, block])
            h1[s] = ring.tile([P, S], F32, name="h1", tag="features", bufs=FEATURE_TILES)
            nc.scalar.activation(h1[s][:], total[:], ACT.Copy, scale=gain_dealt[:, g, t : t + 1])

        w4_w = keep.tile([P, PASSES, 2 * N], U8, align_bytes=64)
        z_codes, z_bytes, score_acc = {}, {}, {}
        free_banks = ["ab"[n % 2] + "%d" % (n // 2) for n in range(8)]
        stage_tags = [("turns", 2), ("whole", 2), ("features", FEATURE_TILES), ("features", FEATURE_TILES)]

        def score_pass(g, m0, width, first):
            tiles = BANK // width
            if g == 0:
                score_acc[m0, first] = bank(free_banks.pop(0), [P, tiles, width])
            for n in range(tiles):
                n0 = (first + n) * P
                nc.tensor.matmul_mx(
                    out=score_acc[m0, first][:, n, :],
                    lhsT=w4_w[:, g, 2 * n0 : 2 * (n0 + P)].bitcast(FP4X4),
                    lhsT_scale=w4_plane[:, g, n0 : n0 + P],
                    rhs=z_codes[g, m0][:].bitcast(FP8X4),
                    rhs_scale=z_bytes[g, m0][:],
                    start=(g == 0 and n == 0),
                    stop=(g == PASSES - 1 and n == tiles - 1),
                )

        def finish_scores(m0, width):
            tiles = BANK // width
            for first in range(0, N // P, tiles):
                score_pass(PASSES - 1, m0, width, first)
                tag, bufs = stage_tags[len(score_acc) % len(stage_tags)]
                staged = ring.tile([P, tiles, width], F32, name="staged", tag=tag, bufs=bufs)
                acc = score_acc.pop((m0, first))
                if m0 + width == T2:
                    nc.vector.tensor_copy(staged[:], acc[:])
                else:
                    nc.scalar.copy(staged[:], acc[:])
                rows = out[first * P : (first + tiles) * P, m0 : m0 + width]
                nc.sync.dma_start(rows.rearrange("(n p) m -> p n m", p=P), staged[:])

        lower, upper = {}, {}

        def place(s):
            g, t = divmod(s, 4)
            page = pa[s % 2]
            nc.vector.tensor_tensor(page[:].indirect(idx3[:]), h1[s][:], wg1_dealt[:, t, :], ALU.mult)
            if t == 0:
                upper[g] = ring.tile([P, 4, T2], F32, name="upper", tag="table", align_bytes=64)
                lower[g] = ring.tile([P, 4, T2], F32, name="lower", tag="rows", bufs=2, align_bytes=64)
            nc.vector.tensor_tensor(upper[g][:, t, :], pb[s][:], lib_rows[s][:], ALU.max)
            nc.vector.tensor_tensor(lower[g][:, t, :], page[:], lib_rows[s][:], ALU.min)
            if t < 3:
                return
            for m0, width in PIECES:
                z = ring.tile([P, 4 * width], BF16, name="z", tag="z", bufs=2, align_bytes=64)
                nc.vector.tensor_tensor(
                    z[:].rearrange("p (c i t) -> p c t i", t=4, i=4),
                    lower[g][:, :, m0 : m0 + width].rearrange("p t (c i) -> p c t i", i=4),
                    upper[g][:, :, m0 : m0 + width].rearrange("p t (c i) -> p c t i", i=4),
                    ALU.add,
                )
                z_codes[g, m0] = keep.tile([P, width], U32, name="z_codes%d_%d" % (g, m0), align_bytes=64)
                z_bytes[g, m0] = keep.tile([P, width], U8, name="z_bytes%d_%d" % (g, m0), align_bytes=64)
                nc.vector.quantize_mx(out=z_codes[g, m0][:].bitcast(FP8X4), scales=z_bytes[g, m0][:], in_=z[:])
                if g == PASSES - 1:
                    finish_scores(m0, width)

        for step in range(SLICES + AHEAD):
            if step < LIB_TILES:
                load_lib(step)
            if step < SLICES:
                shortwave(step)
            if step == 0:
                w_loaded = load_weights(1)
            if step < 2:
                quantise_weight(2 * step, 1, w_loaded[2 * step])
                quantise_weight(2 * step + 1, 1, w_loaded[2 * step + 1])
            if step == 3:
                nc.sync.dma_start(w4_w[:].bitcast(I32), w4_words.rearrange("a p c -> p a c").bitcast(I32))
                for c in range(4):
                    nc.sync.dma_start(
                        w4_plane[32 * c : 32 * c + 4, :, :].bitcast(I32),
                        w4_scales[:, 4 * c : 4 * c + 4, :].rearrange("a r n -> r a n").bitcast(I32),
                    )
            if step == SLICES - 1:
                for m0, width in PIECES:
                    for first in range(0, N // P, BANK // width):
                        score_pass(0, m0, width, first)
            if step >= AHEAD:
                place(step - AHEAD)
                if step - AHEAD + LIB_TILES < SLICES:
                    load_lib(step - AHEAD + LIB_TILES)
